import numpy as np
import ml_dtypes


def mxq(x, axis, fmt="e4m3"):
    dtype, down = {"e4m3": (ml_dtypes.float8_e4m3fn, 7), "e5m2": (ml_dtypes.float8_e5m2, 14)}[fmt]
    v = np.moveaxis(np.asarray(x, np.float32).astype(ml_dtypes.bfloat16).astype(np.float64), axis, -1)
    blocks = v.reshape(v.shape[:-1] + (-1, 32))
    amax = np.abs(blocks).max(-1, keepdims=True)
    byte = np.maximum(np.where(amax > 0, np.frexp(amax)[1] - 1 + 127, 0) - down, 1)
    scale = np.exp2(byte - 127.0)
    codes = (blocks / scale).astype(np.float32).astype(dtype).astype(np.float64)
    return np.moveaxis((codes * scale).reshape(v.shape), -1, axis)


WIDE = False


def mx_kscale(k):
    if not WIDE:
        return np.ones(k)
    levels = np.array([24, -24, 12, -12, 0])
    if k % 512:
        return np.exp2(np.random.permutation(np.resize(levels, k // 32))).repeat(32)
    a = np.empty((k // 512, 16))
    for p in range(k // 512):
        a[p, :8] = np.random.permutation(np.resize(levels, 8))
        for g in range(8):
            far = levels[np.abs(levels - a[p, g]) >= 10]
            a[p, g + 8] = far[np.random.randint(len(far))]
    return np.exp2(a.ravel()).repeat(32)


def f64(x):
    return np.asarray(x).astype(np.float64)


def striped(idx):
    return np.tile(idx.reshape(-1, 16).T, (8, 1)).astype(np.uint16)


def unstriped(offs):
    return offs[:16].T.reshape(-1).astype(np.int64)


E2M1 = np.array([0.0, 0.5, 1.0, 1.5, 2.0, 3.0, 4.0, 6.0, -0.0, -0.5, -1.0, -1.5, -2.0, -3.0, -4.0, -6.0])


def pack_weight(w, fmt):
    k, n = w.shape
    w = f64(np.asarray(w, np.float32).astype(ml_dtypes.bfloat16)).reshape(k // 32, 32, n)
    amax = np.abs(w).max(1)
    if fmt == "e4m3":
        byte = np.frexp(amax)[1] - 1 + 127 - 7
    else:
        mant, ex = np.frexp(amax / 6.0)
        byte = np.where(mant > 0.5, ex, ex - 1) + 127
    byte = np.clip(np.where(amax > 0, byte, 1), 1, 254)
    scaled = (w * np.exp2(127.0 - byte)[:, None, :]).reshape(k, n).astype(np.float32)
    by_word = np.ascontiguousarray(scaled.reshape(k // 512, 128, 4, n).transpose(0, 1, 3, 2))
    if fmt == "e4m3":
        words = by_word.astype(ml_dtypes.float8_e4m3fn).view(np.uint8)
    else:
        c = by_word.astype(ml_dtypes.float4_e2m1fn).view(np.uint8) & 0xF
        words = (c[..., 0::2] | (c[..., 1::2] << 4)).reshape(k // 512, 128, 2 * n)
    return np.ascontiguousarray(words), np.ascontiguousarray(byte.astype(np.uint8).reshape(k // 512, 16, n))


def unpack_weight(words, scales, fmt):
    g, _, n = scales.shape
    words = np.ascontiguousarray(words).reshape(g, 128, n, -1)
    if fmt == "e4m3":
        vals = words.view(ml_dtypes.float8_e4m3fn).astype(np.float64)
    else:
        nib = np.empty((g, 128, n, 4), np.uint8)
        nib[..., 0::2] = words & 0xF
        nib[..., 1::2] = words >> 4
        vals = E2M1[nib]
    vals = vals * np.repeat(np.exp2(scales.astype(np.float64) - 127.0), 8, axis=1)[..., None]
    return vals.transpose(0, 1, 3, 2).reshape(g * 512, n)


K, L, N, T, J = 512, 512, 1024, 1024, 512


def setup_inputs():
    n = np.random.standard_normal
    s = mx_kscale(K)[:, None]
    s2 = mx_kscale(L)[:, None]
    p_tab = pack_weight(n((K, T)) * s, "e4m3")
    p_wt = pack_weight(n((K, N)) / np.sqrt(K) / s, "e2m1")
    p_wx = pack_weight(n((L, N)) / np.sqrt(L) / s2, "e4m3")
    return {
        "tab_words": p_tab[0],
        "tab_scales": p_tab[1],
        "wt_words": p_wt[0],
        "wt_scales": p_wt[1],
        "x": (n((L, J)) * s2).astype(np.float32),
        "wx_words": p_wx[0],
        "wx_scales": p_wx[1],
        "gT": (n((N, T))).astype(np.float32),
        "offs": striped(np.random.permutation(T)[:J]),
    }


def reference(tab_words, tab_scales, wt_words, wt_scales, x, wx_words, wx_scales, gT, offs):
    idx = unstriped(offs)
    tab_ = unpack_weight(tab_words, tab_scales, "e4m3")[:, idx]
    wt_ = unpack_weight(wt_words, wt_scales, "e2m1")
    x_q_ = mxq(f64(x), 0, "e4m3")
    x_r_ = mxq(f64(x) - x_q_, 0, "e4m3")
    wx_ = unpack_weight(wx_words, wx_scales, "e4m3")
    y = wt_.T @ tab_ + wx_.T @ x_q_ + wx_.T @ x_r_
    return y * f64(gT)[:, idx]

@@ -1,0 +1,217 @@
+from contextlib import ExitStack
+
+import concourse.mybir as mybir
+
+K, L, N, T, J = 512, 512, 1024, 1024, 512
+FLOPS = 2 * (K * N * J + 2 * L * N * J + L * L * J)
+
+F32 = mybir.dt.float32
+BF16 = mybir.dt.bfloat16
+I32 = mybir.dt.int32
+U32 = mybir.dt.uint32
+U16 = mybir.dt.uint16
+U8 = mybir.dt.uint8
+FP8X4 = mybir.dt.float8_e4m3fn_x4
+FP4X4 = mybir.dt.float4_e2m1fn_x4
+MULT = mybir.AluOpType.mult
+SUBTRACT = mybir.AluOpType.subtract
+
+P = 128
+PACK = 4
+CHUNK = 128
+CHUNKS = J // CHUNK
+HALF = J // 2
+N_TILES = N // P
+SPLIT_TILES = 2
+
+
+def load_scale_rows(queue, plane, rows):
+    for q in range(4):
+        queue.dma_start(out=plane[32 * q : 32 * q + 4, :].bitcast(I32), in_=rows[4 * q : 4 * q + 4, :].bitcast(I32))
+
+
+def tile_list_tiert_gate_kernel(
+    tc, tab_words, tab_scales, wt_words, wt_scales, x, wx_words, wx_scales, gT, offs, out
+):
+    nc = tc.nc
+    with ExitStack() as ctx:
+        keep = ctx.enter_context(tc.tile_pool(name="keep", bufs=1))
+        reuse = ctx.enter_context(tc.tile_pool(name="reuse", bufs=1))
+        psum = ctx.enter_context(tc.psum_pool(name="psum", bufs=8))
+
+        offsets = keep.tile([P, J // 16], U16, name="offsets")
+        table = keep.tile([P, T], U32, name="table", align_bytes=64)
+        table_sc = keep.tile([P, T], U8, name="table_sc", align_bytes=64)
+        wt = keep.tile([P, 2 * N], U8, name="wt", align_bytes=64)
+        wt_sc = keep.tile([P, N], U8, name="wt_sc", align_bytes=64)
+        wx = keep.tile([P, N], U32, name="wx", align_bytes=64)
+        wx_sc = keep.tile([P, N], U8, name="wx_sc", align_bytes=64)
+        x_raw = [keep.tile([P, PACK, HALF], F32, name="x_raw%d" % h, align_bytes=64) for h in range(2)]
+        gates = [keep.tile([P, T], F32, name="gates%d" % t, align_bytes=64) for t in range(N_TILES)]
+
+        for plane in (table_sc, wx_sc, wt_sc):
+            nc.vector.memset(plane[:].bitcast(I32), 0)
+
+        x_rows = x.rearrange("(p i) j -> p i j", i=PACK)
+
+        def load_gates(t):
+            nc.sync.dma_start(out=gates[t][:], in_=gT[t * P : (t + 1) * P, :])
+
+        nc.sync.dma_start(out=table[:].bitcast(I32), in_=tab_words[0].rearrange("p t i -> p (t i)").bitcast(I32))
+        nc.sync.dma_start(out=offsets[:], in_=offs)
+        load_scale_rows(nc.scalar, table_sc, tab_scales[0])
+        nc.sync.dma_start(out=x_raw[0][:], in_=x_rows[:, :, 0:HALF])
+        nc.sync.dma_start(out=x_raw[1][:], in_=x_rows[:, :, HALF:J])
+        nc.sync.dma_start(out=wx[:].bitcast(I32), in_=wx_words[0].rearrange("p n i -> p (n i)").bitcast(I32))
+        nc.sync.dma_start(out=wt[:].bitcast(I32), in_=wt_words[0].bitcast(I32))
+        load_scale_rows(nc.sync, wx_sc, wx_scales[0])
+        load_gates(0)
+        load_scale_rows(nc.sync, wt_sc, wt_scales[0])
+        for t in range(1, N_TILES):
+            load_gates(t)
+
+        width = P * PACK
+        pick = reuse.tile([P, PACK * width + 32], BF16, name="pick", align_bytes=64, offset=0)
+        last = (PACK - 1) * width
+        source = pick[:, last : last + width + 32]
+        nc.gpsimd.memset(source.bitcast(I32), 0)
+        nc.gpsimd.affine_select(
+            out=source,
+            in_=source,
+            compare_op=mybir.AluOpType.not_equal,
+            fill=1.0,
+            base=PACK - 1,
+            pattern=[[-1, width + 32]],
+            channel_multiplier=PACK,
+        )
+        for i in range(PACK - 1):
+            first = last + PACK - 1 - i
+            nc.vector.tensor_copy(out=pick[:, i * width : (i + 1) * width], in_=pick[:, first : first + width])
+        pick_codes = keep.tile([P, PACK * P], U32, name="pick_codes", align_bytes=64)
+        pick_sc = keep.tile([P, PACK * P], U8, name="pick_sc", align_bytes=64)
+        nc.vector.quantize_mx(
+            out=pick_codes[:].bitcast(FP8X4), scales=pick_sc[:], in_=pick[:, 0 : PACK * width]
+        )
+
+        v_codes = reuse.tile([P, J], U32, name="v_codes", align_bytes=64, offset=0)
+        v_sc = reuse.tile([P, J], U8, name="v_sc", align_bytes=64, offset=8 * J)
+        xq_in = [keep.tile([P, CHUNK, PACK], BF16, name="xq_in%d" % c, align_bytes=64) for c in range(CHUNKS)]
+        xr_in = [keep.tile([P, HALF, PACK], BF16, name="xr_in%d" % h, align_bytes=64) for h in range(2)]
+        xq_codes = reuse.tile([P, J], U32, name="xq_codes", align_bytes=64, offset=4 * J)
+        xq_sc = keep.tile([P, J], U8, name="xq_sc", align_bytes=64)
+        xr_codes = keep.tile([P, J], U32, name="xr_codes", align_bytes=64)
+        xr_sc = keep.tile([P, J], U8, name="xr_sc", align_bytes=64)
+        decoded = {}
+
+        def cols_of(c):
+            return slice(c * CHUNK, (c + 1) * CHUNK)
+
+        def x_chunk(c):
+            inner = (c % 2) * CHUNK
+            return x_raw[c // 2][:, :, inner : inner + CHUNK].rearrange("p i j -> p j i")
+
+        def round_x(c):
+            nc.scalar.copy(out=xq_in[c][:], in_=x_chunk(c))
+
+        def quantize_x(c):
+            nc.vector.quantize_mx(
+                out=xq_codes[:, cols_of(c)].bitcast(FP8X4),
+                scales=xq_sc[:, cols_of(c)],
+                in_=xq_in[c][:].rearrange("p j i -> p (j i)"),
+            )
+            bank = psum.tile([P, PACK, CHUNK], F32, name="bank")
+            decoded[c] = bank
+            for i in range(PACK):
+                m_cols = slice(i * P, (i + 1) * P)
+                nc.tensor.matmul_mx(
+                    out=bank[:, i, :],
+                    lhsT=pick_codes[:, m_cols].bitcast(FP8X4),
+                    lhsT_scale=pick_sc[:, m_cols],
+                    rhs=xq_codes[:, cols_of(c)].bitcast(FP8X4),
+                    rhs_scale=xq_sc[:, cols_of(c)],
+                    start=True,
+                    stop=True,
+                )
+
+        def subtract(c):
+            inner = (c % 2) * CHUNK
+            nc.vector.tensor_tensor(
+                out=xr_in[c // 2][:, inner : inner + CHUNK, :],
+                in0=x_chunk(c),
+                in1=decoded[c][:].rearrange("p i j -> p j i"),
+                op=SUBTRACT,
+            )
+
+        def quantize_rest(h):
+            cols = slice(h * HALF, (h + 1) * HALF)
+            nc.vector.quantize_mx(
+                out=xr_codes[:, cols].bitcast(FP8X4),
+                scales=xr_sc[:, cols],
+                in_=xr_in[h][:].rearrange("p j i -> p (j i)"),
+            )
+
+        def project(acc, t, cols):
+            n_cols = slice(t * P, (t + 1) * P)
+            passes = (
+                (wx[:, n_cols].bitcast(FP8X4), wx_sc, xq_codes, xq_sc),
+                (wt[:, 2 * t * P : 2 * (t + 1) * P].bitcast(FP4X4), wt_sc, v_codes, v_sc),
+                (wx[:, n_cols].bitcast(FP8X4), wx_sc, xr_codes, xr_sc),
+            )
+            for k, (w_codes, w_sc, codes, sc) in enumerate(passes):
+                nc.tensor.matmul_mx(
+                    out=acc,
+                    lhsT=w_codes,
+                    lhsT_scale=w_sc[:, n_cols],
+                    rhs=codes[:, cols].bitcast(FP8X4),
+                    rhs_scale=sc[:, cols],
+                    start=(k == 0),
+                    stop=(k == len(passes) - 1),
+                )
+
+        sums = [keep.tile([P, J], F32, name="sums%d" % t, align_bytes=64) for t in range(N_TILES)]
+        gated = [keep.tile([P, J], F32, name="gated%d" % t, align_bytes=64) for t in range(N_TILES)]
+
+        def sum_part(t, lo, hi):
+            acc = psum.tile([P, J], F32, name="bank")
+            step = J if hi - lo == J else CHUNK
+            for c0 in range(lo, hi, step):
+                project(acc[:, c0 : c0 + step], t, slice(c0, c0 + step))
+            nc.scalar.copy(out=sums[t][:, lo:hi], in_=acc[:, lo:hi])
+
+        def gate_part(t, lo, hi):
+            nc.vector.tensor_tensor(
+                out=gated[t][:, lo:hi],
+                in0=gates[t][:].indirect(offsets[:, lo // 16 : hi // 16]),
+                in1=sums[t][:, lo:hi],
+                op=MULT,
+            )
+
+        def store(t):
+            nc.sync.dma_start(out=out[t * P : (t + 1) * P, :], in_=gated[t][:])
+
+        nc.vector.tensor_copy(out=v_codes[:], in_=table[:].indirect(offsets[:]))
+        for c in range(CHUNKS):
+            round_x(c)
+        nc.vector.tensor_copy(out=v_sc[:], in_=table_sc[:].indirect(offsets[:]))
+        quantize_x(0)
+        quantize_x(1)
+        quantize_x(2)
+        subtract(0)
+        quantize_x(3)
+        subtract(1)
+        subtract(2)
+        quantize_rest(0)
+        for t in range(SPLIT_TILES):
+            sum_part(t, 0, HALF)
+        subtract(3)
+        quantize_rest(1)
+        for t in range(SPLIT_TILES):
+            gate_part(t, 0, HALF)
+        for t in range(SPLIT_TILES):
+            sum_part(t, HALF, J)
+            gate_part(t, HALF, J)
+            store(t)
+        for t in range(SPLIT_TILES, N_TILES):
+            sum_part(t, 0, J)
+            gate_part(t, 0, J)
+            store(t)

@@ -22,7 +22,7 @@ CHUNK = 128
 CHUNKS = J // CHUNK
 HALF = J // 2
 N_TILES = N // P
-SPLIT_TILES = 2
+SPLIT_TILES = 3
 
 
 def load_scale_rows(queue, plane, rows):
@@ -57,17 +57,16 @@ def tile_list_tiert_gate_kernel(
         def load_gates(t):
             nc.sync.dma_start(out=gates[t][:], in_=gT[t * P : (t + 1) * P, :])
 
-        nc.sync.dma_start(out=table[:].bitcast(I32), in_=tab_words[0].rearrange("p t i -> p (t i)").bitcast(I32))
+        nc.sync.dma_start(out=x_raw[0][:], in_=x_rows[:, :, 0:HALF])
         nc.sync.dma_start(out=offsets[:], in_=offs)
         load_scale_rows(nc.scalar, table_sc, tab_scales[0])
-        nc.sync.dma_start(out=x_raw[0][:], in_=x_rows[:, :, 0:HALF])
+        nc.sync.dma_start(out=table[:].bitcast(I32), in_=tab_words[0].rearrange("p t i -> p (t i)").bitcast(I32))
         nc.sync.dma_start(out=x_raw[1][:], in_=x_rows[:, :, HALF:J])
+        load_scale_rows(nc.sync, wx_sc, wx_scales[0])
         nc.sync.dma_start(out=wx[:].bitcast(I32), in_=wx_words[0].rearrange("p n i -> p (n i)").bitcast(I32))
         nc.sync.dma_start(out=wt[:].bitcast(I32), in_=wt_words[0].bitcast(I32))
-        load_scale_rows(nc.sync, wx_sc, wx_scales[0])
-        load_gates(0)
         load_scale_rows(nc.sync, wt_sc, wt_scales[0])
-        for t in range(1, N_TILES):
+        for t in range(N_TILES):
             load_gates(t)
 
         width = P * PACK
@@ -76,13 +75,13 @@ def tile_list_tiert_gate_kernel(
         source = pick[:, last : last + width + 32]
         nc.gpsimd.memset(source.bitcast(I32), 0)
         nc.gpsimd.affine_select(
-            out=source,
-            in_=source,
+            out=source.bitcast(F32),
+            in_=source.bitcast(F32),
             compare_op=mybir.AluOpType.not_equal,
             fill=1.0,
-            base=PACK - 1,
-            pattern=[[-1, width + 32]],
-            channel_multiplier=PACK,
+            base=1,
+            pattern=[[-1, (width + 32) // 2]],
+            channel_multiplier=2,
         )
         for i in range(PACK - 1):
             first = last + PACK - 1 - i
@@ -108,10 +107,10 @@ def tile_list_tiert_gate_kernel(
 
         def x_chunk(c):
             inner = (c % 2) * CHUNK
-            return x_raw[c // 2][:, :, inner : inner + CHUNK].rearrange("p i j -> p j i")
+            return x_raw[c // 2][:, :, inner : inner + CHUNK].rearrange("p i (g e) -> p g i e", e=4)
 
         def round_x(c):
-            nc.scalar.copy(out=xq_in[c][:], in_=x_chunk(c))
+            nc.scalar.copy(out=xq_in[c][:].rearrange("p (g e) i -> p g i e", e=4), in_=x_chunk(c))
 
         def quantize_x(c):
             nc.vector.quantize_mx(
@@ -136,9 +135,9 @@ def tile_list_tiert_gate_kernel(
         def subtract(c):
             inner = (c % 2) * CHUNK
             nc.vector.tensor_tensor(
-                out=xr_in[c // 2][:, inner : inner + CHUNK, :],
+                out=xr_in[c // 2][:, inner : inner + CHUNK, :].rearrange("p (g e) i -> p g i e", e=4),
                 in0=x_chunk(c),
-                in1=decoded[c][:].rearrange("p i j -> p j i"),
+                in1=decoded[c][:].rearrange("p i (g e) -> p g i e", e=4),
                 op=SUBTRACT,
             )
 
@@ -150,16 +149,17 @@ def tile_list_tiert_gate_kernel(
                 in_=xr_in[h][:].rearrange("p j i -> p (j i)"),
             )
 
-        def project(acc, t, cols):
+        def project(acc, t, lo, hi):
             n_cols = slice(t * P, (t + 1) * P)
-            passes = (
-                (wx[:, n_cols].bitcast(FP8X4), wx_sc, xq_codes, xq_sc),
-                (wt[:, 2 * t * P : 2 * (t + 1) * P].bitcast(FP4X4), wt_sc, v_codes, v_sc),
-                (wx[:, n_cols].bitcast(FP8X4), wx_sc, xr_codes, xr_sc),
-            )
-            for k, (w_codes, w_sc, codes, sc) in enumerate(passes):
+            wx_codes = wx[:, n_cols].bitcast(FP8X4)
+            wt_codes = wt[:, 2 * t * P : 2 * (t + 1) * P].bitcast(FP4X4)
+            step = J if hi - lo == J else CHUNK
+            passes = [(wx_codes, wx_sc, xq_codes, xq_sc, slice(lo, hi))]
+            passes += [(wt_codes, wt_sc, v_codes, v_sc, slice(c0, c0 + step)) for c0 in range(lo, hi, step)]
+            passes += [(wx_codes, wx_sc, xr_codes, xr_sc, slice(lo, hi))]
+            for k, (w_codes, w_sc, codes, sc, cols) in enumerate(passes):
                 nc.tensor.matmul_mx(
-                    out=acc,
+                    out=acc[:, cols],
                     lhsT=w_codes,
                     lhsT_scale=w_sc[:, n_cols],
                     rhs=codes[:, cols].bitcast(FP8X4),
@@ -173,9 +173,7 @@ def tile_list_tiert_gate_kernel(
 
         def sum_part(t, lo, hi):
             acc = psum.tile([P, J], F32, name="bank")
-            step = J if hi - lo == J else CHUNK
-            for c0 in range(lo, hi, step):
-                project(acc[:, c0 : c0 + step], t, slice(c0, c0 + step))
+            project(acc, t, lo, hi)
             nc.scalar.copy(out=sums[t][:, lo:hi], in_=acc[:, lo:hi])
 
         def gate_part(t, lo, hi):
@@ -189,23 +187,24 @@ def tile_list_tiert_gate_kernel(
         def store(t):
             nc.sync.dma_start(out=out[t * P : (t + 1) * P, :], in_=gated[t][:])
 
-        nc.vector.tensor_copy(out=v_codes[:], in_=table[:].indirect(offsets[:]))
         for c in range(CHUNKS):
             round_x(c)
         nc.vector.tensor_copy(out=v_sc[:], in_=table_sc[:].indirect(offsets[:]))
         quantize_x(0)
         quantize_x(1)
-        quantize_x(2)
+        nc.vector.tensor_copy(out=v_codes[:], in_=table[:].indirect(offsets[:]))
         subtract(0)
-        quantize_x(3)
+        quantize_x(2)
         subtract(1)
-        subtract(2)
+        quantize_x(3)
         quantize_rest(0)
         for t in range(SPLIT_TILES):
             sum_part(t, 0, HALF)
+        subtract(2)
         subtract(3)
+        gate_part(0, 0, HALF)
         quantize_rest(1)
-        for t in range(SPLIT_TILES):
+        for t in range(1, SPLIT_TILES):
             gate_part(t, 0, HALF)
         for t in range(SPLIT_TILES):
             sum_part(t, HALF, J)

@@ -25,9 +25,9 @@ N_TILES = N // P
 SPLIT_TILES = 3
 
 
-def load_scale_rows(queue, plane, rows):
-    for q in range(4):
-        queue.dma_start(out=plane[32 * q : 32 * q + 4, :].bitcast(I32), in_=rows[4 * q : 4 * q + 4, :].bitcast(I32))
+def load_scale_rows(queue, plane, rows, first):
+    for r in range(4):
+        queue.dma_start(out=plane[first + r : P : 32, :].bitcast(I32), in_=rows[r:16:4, :].bitcast(I32))
 
 
 def tile_list_tiert_gate_kernel(
@@ -43,13 +43,12 @@ def tile_list_tiert_gate_kernel(
         table = keep.tile([P, T], U32, name="table", align_bytes=64)
         table_sc = keep.tile([P, T], U8, name="table_sc", align_bytes=64)
         wt = keep.tile([P, 2 * N], U8, name="wt", align_bytes=64)
-        wt_sc = keep.tile([P, N], U8, name="wt_sc", align_bytes=64)
+        w_sc = keep.tile([P, N], U8, name="w_sc", align_bytes=64)
         wx = keep.tile([P, N], U32, name="wx", align_bytes=64)
-        wx_sc = keep.tile([P, N], U8, name="wx_sc", align_bytes=64)
         x_raw = [keep.tile([P, PACK, HALF], F32, name="x_raw%d" % h, align_bytes=64) for h in range(2)]
         gates = [keep.tile([P, T], F32, name="gates%d" % t, align_bytes=64) for t in range(N_TILES)]
 
-        for plane in (table_sc, wx_sc, wt_sc):
+        for plane in (table_sc, w_sc):
             nc.vector.memset(plane[:].bitcast(I32), 0)
 
         x_rows = x.rearrange("(p i) j -> p i j", i=PACK)
@@ -57,15 +56,15 @@ def tile_list_tiert_gate_kernel(
         def load_gates(t):
             nc.sync.dma_start(out=gates[t][:], in_=gT[t * P : (t + 1) * P, :])
 
-        nc.sync.dma_start(out=x_raw[0][:], in_=x_rows[:, :, 0:HALF])
         nc.sync.dma_start(out=offsets[:], in_=offs)
-        load_scale_rows(nc.scalar, table_sc, tab_scales[0])
+        load_scale_rows(nc.scalar, table_sc, tab_scales[0], 0)
+        nc.sync.dma_start(out=x_raw[0][:], in_=x_rows[:, :, 0:HALF])
         nc.sync.dma_start(out=table[:].bitcast(I32), in_=tab_words[0].rearrange("p t i -> p (t i)").bitcast(I32))
         nc.sync.dma_start(out=x_raw[1][:], in_=x_rows[:, :, HALF:J])
-        load_scale_rows(nc.sync, wx_sc, wx_scales[0])
-        nc.sync.dma_start(out=wx[:].bitcast(I32), in_=wx_words[0].rearrange("p n i -> p (n i)").bitcast(I32))
         nc.sync.dma_start(out=wt[:].bitcast(I32), in_=wt_words[0].bitcast(I32))
-        load_scale_rows(nc.sync, wt_sc, wt_scales[0])
+        load_scale_rows(nc.sync, w_sc, wt_scales[0], 0)
+        nc.sync.dma_start(out=wx[:].bitcast(I32), in_=wx_words[0].rearrange("p n i -> p (n i)").bitcast(I32))
+        load_scale_rows(nc.sync, w_sc, wx_scales[0], 4)
         for t in range(N_TILES):
             load_gates(t)
 
@@ -154,14 +153,14 @@ def tile_list_tiert_gate_kernel(
             wx_codes = wx[:, n_cols].bitcast(FP8X4)
             wt_codes = wt[:, 2 * t * P : 2 * (t + 1) * P].bitcast(FP4X4)
             step = J if hi - lo == J else CHUNK
-            passes = [(wx_codes, wx_sc, xq_codes, xq_sc, slice(lo, hi))]
-            passes += [(wt_codes, wt_sc, v_codes, v_sc, slice(c0, c0 + step)) for c0 in range(lo, hi, step)]
-            passes += [(wx_codes, wx_sc, xr_codes, xr_sc, slice(lo, hi))]
-            for k, (w_codes, w_sc, codes, sc, cols) in enumerate(passes):
+            passes = [(wx_codes, 4, xq_codes, xq_sc, slice(lo, hi))]
+            passes += [(wt_codes, 0, v_codes, v_sc, slice(c0, c0 + step)) for c0 in range(lo, hi, step)]
+            passes += [(wx_codes, 4, xr_codes, xr_sc, slice(lo, hi))]
+            for k, (w_codes, first, codes, sc, cols) in enumerate(passes):
                 nc.tensor.matmul_mx(
                     out=acc[:, cols],
                     lhsT=w_codes,
-                    lhsT_scale=w_sc[:, n_cols],
+                    lhsT_scale=w_sc[first:P, n_cols],
                     rhs=codes[:, cols].bitcast(FP8X4),
                     rhs_scale=sc[:, cols],
                     start=(k == 0),

@@ -22,7 +22,7 @@ CHUNK = 128
 CHUNKS = J // CHUNK
 HALF = J // 2
 N_TILES = N // P
-SPLIT_TILES = 3
+EARLY = 3 * CHUNK
 
 
 def load_scale_rows(queue, plane, rows, first):
@@ -56,16 +56,17 @@ def tile_list_tiert_gate_kernel(
         def load_gates(t):
             nc.sync.dma_start(out=gates[t][:], in_=gT[t * P : (t + 1) * P, :])
 
-        nc.sync.dma_start(out=offsets[:], in_=offs)
-        load_scale_rows(nc.scalar, table_sc, tab_scales[0], 0)
         nc.sync.dma_start(out=x_raw[0][:], in_=x_rows[:, :, 0:HALF])
+        nc.sync.dma_start(out=offsets[:], in_=offs)
+        load_scale_rows(nc.sync, table_sc, tab_scales[0], 0)
         nc.sync.dma_start(out=table[:].bitcast(I32), in_=tab_words[0].rearrange("p t i -> p (t i)").bitcast(I32))
         nc.sync.dma_start(out=x_raw[1][:], in_=x_rows[:, :, HALF:J])
         nc.sync.dma_start(out=wt[:].bitcast(I32), in_=wt_words[0].bitcast(I32))
         load_scale_rows(nc.sync, w_sc, wt_scales[0], 0)
         nc.sync.dma_start(out=wx[:].bitcast(I32), in_=wx_words[0].rearrange("p n i -> p (n i)").bitcast(I32))
+        load_gates(0)
         load_scale_rows(nc.sync, w_sc, wx_scales[0], 4)
-        for t in range(N_TILES):
+        for t in range(1, N_TILES):
             load_gates(t)
 
         width = P * PACK
@@ -94,7 +95,7 @@ def tile_list_tiert_gate_kernel(
         v_codes = reuse.tile([P, J], U32, name="v_codes", align_bytes=64, offset=0)
         v_sc = reuse.tile([P, J], U8, name="v_sc", align_bytes=64, offset=8 * J)
         xq_in = [keep.tile([P, CHUNK, PACK], BF16, name="xq_in%d" % c, align_bytes=64) for c in range(CHUNKS)]
-        xr_in = [keep.tile([P, HALF, PACK], BF16, name="xr_in%d" % h, align_bytes=64) for h in range(2)]
+        xr_in = keep.tile([P, J, PACK], BF16, name="xr_in", align_bytes=64)
         xq_codes = reuse.tile([P, J], U32, name="xq_codes", align_bytes=64, offset=4 * J)
         xq_sc = keep.tile([P, J], U8, name="xq_sc", align_bytes=64)
         xr_codes = keep.tile([P, J], U32, name="xr_codes", align_bytes=64)
@@ -132,20 +133,19 @@ def tile_list_tiert_gate_kernel(
                 )
 
         def subtract(c):
-            inner = (c % 2) * CHUNK
             nc.vector.tensor_tensor(
-                out=xr_in[c // 2][:, inner : inner + CHUNK, :].rearrange("p (g e) i -> p g i e", e=4),
+                out=xr_in[:, cols_of(c), :].rearrange("p (g e) i -> p g i e", e=4),
                 in0=x_chunk(c),
                 in1=decoded[c][:].rearrange("p i (g e) -> p g i e", e=4),
                 op=SUBTRACT,
             )
 
-        def quantize_rest(h):
-            cols = slice(h * HALF, (h + 1) * HALF)
+        def quantize_rest(lo, hi):
+            cols = slice(lo, hi)
             nc.vector.quantize_mx(
                 out=xr_codes[:, cols].bitcast(FP8X4),
                 scales=xr_sc[:, cols],
-                in_=xr_in[h][:].rearrange("p j i -> p (j i)"),
+                in_=xr_in[:, cols, :].rearrange("p j i -> p (j i)"),
             )
 
         def project(acc, t, lo, hi):
@@ -170,9 +170,11 @@ def tile_list_tiert_gate_kernel(
         sums = [keep.tile([P, J], F32, name="sums%d" % t, align_bytes=64) for t in range(N_TILES)]
         gated = [keep.tile([P, J], F32, name="gated%d" % t, align_bytes=64) for t in range(N_TILES)]
 
-        def sum_part(t, lo, hi):
+        def sum_part(t, *edges):
             acc = psum.tile([P, J], F32, name="bank")
-            project(acc, t, lo, hi)
+            lo, hi = edges[0], edges[-1]
+            for k in range(len(edges) - 1):
+                project(acc, t, edges[k], edges[k + 1])
             nc.scalar.copy(out=sums[t][:, lo:hi], in_=acc[:, lo:hi])
 
         def gate_part(t, lo, hi):
@@ -196,20 +198,17 @@ def tile_list_tiert_gate_kernel(
         quantize_x(2)
         subtract(1)
         quantize_x(3)
-        quantize_rest(0)
-        for t in range(SPLIT_TILES):
-            sum_part(t, 0, HALF)
         subtract(2)
+        quantize_rest(0, HALF)
+        quantize_rest(HALF, EARLY)
+        sum_part(0, 0, HALF, EARLY)
         subtract(3)
-        gate_part(0, 0, HALF)
-        quantize_rest(1)
-        for t in range(1, SPLIT_TILES):
-            gate_part(t, 0, HALF)
-        for t in range(SPLIT_TILES):
-            sum_part(t, HALF, J)
-            gate_part(t, HALF, J)
-            store(t)
-        for t in range(SPLIT_TILES, N_TILES):
+        quantize_rest(EARLY, J)
+        gate_part(0, 0, EARLY)
+        sum_part(0, EARLY, J)
+        gate_part(0, EARLY, J)
+        store(0)
+        for t in range(1, N_TILES):
             sum_part(t, 0, J)
             gate_part(t, 0, J)
             store(t)

@@ -22,7 +22,9 @@ CHUNK = 128
 CHUNKS = J // CHUNK
 HALF = J // 2
 N_TILES = N // P
-EARLY = 3 * CHUNK
+SPLIT = 2
+WARM = 3
+TAIL = CHUNK
 
 
 def load_scale_rows(queue, plane, rows, first):
@@ -61,12 +63,11 @@ def tile_list_tiert_gate_kernel(
         load_scale_rows(nc.sync, table_sc, tab_scales[0], 0)
         nc.sync.dma_start(out=table[:].bitcast(I32), in_=tab_words[0].rearrange("p t i -> p (t i)").bitcast(I32))
         nc.sync.dma_start(out=x_raw[1][:], in_=x_rows[:, :, HALF:J])
+        load_scale_rows(nc.sync, w_sc, wx_scales[0], 4)
+        nc.sync.dma_start(out=wx[:].bitcast(I32), in_=wx_words[0].rearrange("p n i -> p (n i)").bitcast(I32))
         nc.sync.dma_start(out=wt[:].bitcast(I32), in_=wt_words[0].bitcast(I32))
         load_scale_rows(nc.sync, w_sc, wt_scales[0], 0)
-        nc.sync.dma_start(out=wx[:].bitcast(I32), in_=wx_words[0].rearrange("p n i -> p (n i)").bitcast(I32))
-        load_gates(0)
-        load_scale_rows(nc.sync, w_sc, wx_scales[0], 4)
-        for t in range(1, N_TILES):
+        for t in range(N_TILES):
             load_gates(t)
 
         width = P * PACK
@@ -185,30 +186,43 @@ def tile_list_tiert_gate_kernel(
                 op=MULT,
             )
 
-        def store(t):
-            nc.sync.dma_start(out=out[t * P : (t + 1) * P, :], in_=gated[t][:])
+        def store(t, lo, hi):
+            nc.sync.dma_start(out=out[t * P : (t + 1) * P, lo:hi], in_=gated[t][:, lo:hi])
 
         for c in range(CHUNKS):
             round_x(c)
         nc.vector.tensor_copy(out=v_sc[:], in_=table_sc[:].indirect(offsets[:]))
         quantize_x(0)
         quantize_x(1)
+        warm = psum.tile([P, 2, HALF], F32, name="bank")
+        for k in range(WARM):
+            nc.tensor.matmul_mx(
+                out=warm[:, k % 2, :],
+                lhsT=pick_codes[:, 0:P].bitcast(FP8X4),
+                lhsT_scale=pick_sc[:, 0:P],
+                rhs=xq_codes[:, 0:HALF].bitcast(FP8X4),
+                rhs_scale=xq_sc[:, 0:HALF],
+                start=True,
+                stop=True,
+            )
         nc.vector.tensor_copy(out=v_codes[:], in_=table[:].indirect(offsets[:]))
-        subtract(0)
         quantize_x(2)
-        subtract(1)
+        subtract(0)
         quantize_x(3)
+        subtract(1)
         subtract(2)
         quantize_rest(0, HALF)
-        quantize_rest(HALF, EARLY)
-        sum_part(0, 0, HALF, EARLY)
         subtract(3)
-        quantize_rest(EARLY, J)
-        gate_part(0, 0, EARLY)
-        sum_part(0, EARLY, J)
-        gate_part(0, EARLY, J)
-        store(0)
-        for t in range(1, N_TILES):
+        quantize_rest(HALF, J)
+        for lo in (0, HALF):
+            for t in range(SPLIT):
+                sum_part(t, lo, lo + HALF)
+                gate_part(t, lo, lo + HALF)
+                if lo:
+                    store(t, 0, J)
+        for t in range(SPLIT, N_TILES):
             sum_part(t, 0, J)
-            gate_part(t, 0, J)
-            store(t)
+            edges = (0, J - TAIL, J) if t == N_TILES - 1 else (0, J)
+            for k in range(len(edges) - 1):
+                gate_part(t, edges[k], edges[k + 1])
+                store(t, edges[k], edges[k + 1])

@@ -22,6 +22,7 @@ CHUNK = 128
 CHUNKS = J // CHUNK
 HALF = J // 2
 N_TILES = N // P
+STORE_GROUPS = ((0, 4), (4, 2), (6, 1), (7, 1))
 SPLIT = 2
 WARM = 3
 TAIL = CHUNK
@@ -169,7 +170,11 @@ def tile_list_tiert_gate_kernel(
                 )
 
         sums = [keep.tile([P, J], F32, name="sums%d" % t, align_bytes=64) for t in range(N_TILES)]
-        gated = [keep.tile([P, J], F32, name="gated%d" % t, align_bytes=64) for t in range(N_TILES)]
+        gated = {}
+        for first, count in STORE_GROUPS:
+            group = keep.tile([P, count, J], F32, name="gated%d" % first, align_bytes=64)
+            for k in range(count):
+                gated[first + k] = (group, first, count)
 
         def sum_part(t, *edges):
             acc = psum.tile([P, J], F32, name="bank")
@@ -180,14 +185,17 @@ def tile_list_tiert_gate_kernel(
 
         def gate_part(t, lo, hi):
             nc.vector.tensor_tensor(
-                out=gated[t][:, lo:hi],
+                out=gated[t][0][:, t - gated[t][1], lo:hi],
                 in0=gates[t][:].indirect(offsets[:, lo // 16 : hi // 16]),
                 in1=sums[t][:, lo:hi],
                 op=MULT,
             )
 
         def store(t, lo, hi):
-            nc.sync.dma_start(out=out[t * P : (t + 1) * P, lo:hi], in_=gated[t][:, lo:hi])
+            group, first, count = gated[t]
+            if t == first + count - 1:
+                rows = out[first * P : (first + count) * P, lo:hi].rearrange("(g p) j -> p g j", p=P)
+                nc.sync.dma_start(out=rows, in_=group[:, :, lo:hi])
 
         for c in range(CHUNKS):
             round_x(c)

@@ -107,12 +107,12 @@ def tile_list_tiert_gate_kernel(
         def cols_of(c):
             return slice(c * CHUNK, (c + 1) * CHUNK)
 
-        def x_chunk(c):
+        def x_chunk(c, run):
             inner = (c % 2) * CHUNK
-            return x_raw[c // 2][:, :, inner : inner + CHUNK].rearrange("p i (g e) -> p g i e", e=4)
+            return x_raw[c // 2][:, :, inner : inner + CHUNK].rearrange("p i (g e) -> p g i e", e=run)
 
         def round_x(c):
-            nc.scalar.copy(out=xq_in[c][:].rearrange("p (g e) i -> p g i e", e=4), in_=x_chunk(c))
+            nc.scalar.copy(out=xq_in[c][:].rearrange("p (g e) i -> p g i e", e=4), in_=x_chunk(c, 4))
 
         def quantize_x(c):
             nc.vector.quantize_mx(
@@ -136,9 +136,9 @@ def tile_list_tiert_gate_kernel(
 
         def subtract(c):
             nc.vector.tensor_tensor(
-                out=xr_in[:, cols_of(c), :].rearrange("p (g e) i -> p g i e", e=4),
-                in0=x_chunk(c),
-                in1=decoded[c][:].rearrange("p i (g e) -> p g i e", e=4),
+                out=xr_in[:, cols_of(c), :].rearrange("p (g e) i -> p g i e", e=2),
+                in0=x_chunk(c, 2),
+                in1=decoded[c][:].rearrange("p i (g e) -> p g i e", e=2),
                 op=SUBTRACT,
             )
 

@@ -23,7 +23,8 @@ CHUNKS = J // CHUNK
 HALF = J // 2
 N_TILES = N // P
 STORE_GROUPS = ((0, 4), (4, 2), (6, 1), (7, 1))
-SPLIT = 2
+EARLY = 3 * CHUNK
+GATES_AHEAD = 3
 WARM = 3
 TAIL = CHUNK
 
@@ -40,6 +41,7 @@ def tile_list_tiert_gate_kernel(
     with ExitStack() as ctx:
         keep = ctx.enter_context(tc.tile_pool(name="keep", bufs=1))
         reuse = ctx.enter_context(tc.tile_pool(name="reuse", bufs=1))
+        ring = ctx.enter_context(tc.tile_pool(name="ring", bufs=2))
         psum = ctx.enter_context(tc.psum_pool(name="psum", bufs=8))
 
         offsets = keep.tile([P, J // 16], U16, name="offsets")
@@ -47,7 +49,7 @@ def tile_list_tiert_gate_kernel(
         table_sc = keep.tile([P, T], U8, name="table_sc", align_bytes=64)
         wt = keep.tile([P, 2 * N], U8, name="wt", align_bytes=64)
         w_sc = keep.tile([P, N], U8, name="w_sc", align_bytes=64)
-        wx = keep.tile([P, N], U32, name="wx", align_bytes=64)
+        wx = [keep.tile([P, N // 2], U32, name="wx%d" % h, align_bytes=64) for h in range(2)]
         x_raw = [keep.tile([P, PACK, HALF], F32, name="x_raw%d" % h, align_bytes=64) for h in range(2)]
         gates = [keep.tile([P, T], F32, name="gates%d" % t, align_bytes=64) for t in range(N_TILES)]
 
@@ -59,16 +61,22 @@ def tile_list_tiert_gate_kernel(
         def load_gates(t):
             nc.sync.dma_start(out=gates[t][:], in_=gT[t * P : (t + 1) * P, :])
 
+        def load_wx(h):
+            wx_rows = wx_words[0].rearrange("p n i -> p (n i)").bitcast(I32)
+            nc.sync.dma_start(out=wx[h][:].bitcast(I32), in_=wx_rows[:, h * N // 2 : (h + 1) * N // 2])
+
         nc.sync.dma_start(out=x_raw[0][:], in_=x_rows[:, :, 0:HALF])
         nc.sync.dma_start(out=offsets[:], in_=offs)
         load_scale_rows(nc.sync, table_sc, tab_scales[0], 0)
         nc.sync.dma_start(out=table[:].bitcast(I32), in_=tab_words[0].rearrange("p t i -> p (t i)").bitcast(I32))
         nc.sync.dma_start(out=x_raw[1][:], in_=x_rows[:, :, HALF:J])
         load_scale_rows(nc.sync, w_sc, wx_scales[0], 4)
-        nc.sync.dma_start(out=wx[:].bitcast(I32), in_=wx_words[0].rearrange("p n i -> p (n i)").bitcast(I32))
+        load_wx(0)
         nc.sync.dma_start(out=wt[:].bitcast(I32), in_=wt_words[0].bitcast(I32))
         load_scale_rows(nc.sync, w_sc, wt_scales[0], 0)
         for t in range(N_TILES):
+            if t == GATES_AHEAD:
+                load_wx(1)
             load_gates(t)
 
         width = P * PACK
@@ -96,7 +104,7 @@ def tile_list_tiert_gate_kernel(
 
         v_codes = reuse.tile([P, J], U32, name="v_codes", align_bytes=64, offset=0)
         v_sc = reuse.tile([P, J], U8, name="v_sc", align_bytes=64, offset=8 * J)
-        xq_in = [keep.tile([P, CHUNK, PACK], BF16, name="xq_in%d" % c, align_bytes=64) for c in range(CHUNKS)]
+        xq_in = {}
         xr_in = keep.tile([P, J, PACK], BF16, name="xr_in", align_bytes=64)
         xq_codes = reuse.tile([P, J], U32, name="xq_codes", align_bytes=64, offset=4 * J)
         xq_sc = keep.tile([P, J], U8, name="xq_sc", align_bytes=64)
@@ -112,6 +120,7 @@ def tile_list_tiert_gate_kernel(
             return x_raw[c // 2][:, :, inner : inner + CHUNK].rearrange("p i (g e) -> p g i e", e=run)
 
         def round_x(c):
+            xq_in[c] = ring.tile([P, CHUNK, PACK], BF16, name="xq_in", align_bytes=64)
             nc.scalar.copy(out=xq_in[c][:].rearrange("p (g e) i -> p g i e", e=4), in_=x_chunk(c, 4))
 
         def quantize_x(c):
@@ -152,12 +161,14 @@ def tile_list_tiert_gate_kernel(
 
         def project(acc, t, lo, hi):
             n_cols = slice(t * P, (t + 1) * P)
-            wx_codes = wx[:, n_cols].bitcast(FP8X4)
+            h, inner = divmod(t, N_TILES // 2)
+            wx_codes = wx[h][:, inner * P : (inner + 1) * P].bitcast(FP8X4)
             wt_codes = wt[:, 2 * t * P : 2 * (t + 1) * P].bitcast(FP4X4)
             step = J if hi - lo == J else CHUNK
-            passes = [(wx_codes, 4, xq_codes, xq_sc, slice(lo, hi))]
+            wide = [slice(lo, hi)] if hi - lo != EARLY else [slice(0, HALF), slice(HALF, EARLY)]
+            passes = [(wx_codes, 4, xq_codes, xq_sc, cols) for cols in wide]
             passes += [(wt_codes, 0, v_codes, v_sc, slice(c0, c0 + step)) for c0 in range(lo, hi, step)]
-            passes += [(wx_codes, 4, xr_codes, xr_sc, slice(lo, hi))]
+            passes += [(wx_codes, 4, xr_codes, xr_sc, cols) for cols in wide]
             for k, (w_codes, first, codes, sc, cols) in enumerate(passes):
                 nc.tensor.matmul_mx(
                     out=acc[:, cols],
@@ -197,8 +208,8 @@ def tile_list_tiert_gate_kernel(
                 rows = out[first * P : (first + count) * P, lo:hi].rearrange("(g p) j -> p g j", p=P)
                 nc.sync.dma_start(out=rows, in_=group[:, :, lo:hi])
 
-        for c in range(CHUNKS):
-            round_x(c)
+        round_x(0)
+        round_x(1)
         nc.vector.tensor_copy(out=v_sc[:], in_=table_sc[:].indirect(offsets[:]))
         quantize_x(0)
         quantize_x(1)
@@ -213,22 +224,27 @@ def tile_list_tiert_gate_kernel(
                 start=True,
                 stop=True,
             )
+        round_x(2)
+        round_x(3)
         nc.vector.tensor_copy(out=v_codes[:], in_=table[:].indirect(offsets[:]))
-        quantize_x(2)
         subtract(0)
-        quantize_x(3)
+        quantize_x(2)
         subtract(1)
+        quantize_x(3)
         subtract(2)
         quantize_rest(0, HALF)
+        quantize_rest(HALF, EARLY)
         subtract(3)
-        quantize_rest(HALF, J)
-        for lo in (0, HALF):
-            for t in range(SPLIT):
-                sum_part(t, lo, lo + HALF)
-                gate_part(t, lo, lo + HALF)
-                if lo:
-                    store(t, 0, J)
-        for t in range(SPLIT, N_TILES):
+        quantize_rest(EARLY, J)
+        sum_part(0, 0, HALF)
+        sum_part(0, HALF, EARLY)
+        sum_part(1, 0, EARLY)
+        sum_part(0, EARLY, J)
+        sum_part(1, EARLY, J)
+        gate_part(0, 0, EARLY)
+        gate_part(0, EARLY, J)
+        gate_part(1, 0, J)
+        for t in range(2, N_TILES):
             sum_part(t, 0, J)
             edges = (0, J - TAIL, J) if t == N_TILES - 1 else (0, J)
             for k in range(len(edges) - 1):

@@ -25,7 +25,6 @@ N_TILES = N // P
 STORE_GROUPS = ((0, 4), (4, 2), (6, 1), (7, 1))
 EARLY = 3 * CHUNK
 GATES_AHEAD = 3
-WARM = 3
 TAIL = CHUNK
 
 
@@ -213,17 +212,6 @@ def tile_list_tiert_gate_kernel(
         nc.vector.tensor_copy(out=v_sc[:], in_=table_sc[:].indirect(offsets[:]))
         quantize_x(0)
         quantize_x(1)
-        warm = psum.tile([P, 2, HALF], F32, name="bank")
-        for k in range(WARM):
-            nc.tensor.matmul_mx(
-                out=warm[:, k % 2, :],
-                lhsT=pick_codes[:, 0:P].bitcast(FP8X4),
-                lhsT_scale=pick_sc[:, 0:P],
-                rhs=xq_codes[:, 0:HALF].bitcast(FP8X4),
-                rhs_scale=xq_sc[:, 0:HALF],
-                start=True,
-                stop=True,
-            )
         round_x(2)
         round_x(3)
         nc.vector.tensor_copy(out=v_codes[:], in_=table[:].indirect(offsets[:]))

@@ -40,7 +40,6 @@ def tile_list_tiert_gate_kernel(
     with ExitStack() as ctx:
         keep = ctx.enter_context(tc.tile_pool(name="keep", bufs=1))
         reuse = ctx.enter_context(tc.tile_pool(name="reuse", bufs=1))
-        ring = ctx.enter_context(tc.tile_pool(name="ring", bufs=2))
         psum = ctx.enter_context(tc.psum_pool(name="psum", bufs=8))
 
         offsets = keep.tile([P, J // 16], U16, name="offsets")
@@ -103,7 +102,7 @@ def tile_list_tiert_gate_kernel(
 
         v_codes = reuse.tile([P, J], U32, name="v_codes", align_bytes=64, offset=0)
         v_sc = reuse.tile([P, J], U8, name="v_sc", align_bytes=64, offset=8 * J)
-        xq_in = {}
+        xq_in = keep.tile([P, HALF, PACK], BF16, name="xq_in", align_bytes=64)
         xr_in = keep.tile([P, J, PACK], BF16, name="xr_in", align_bytes=64)
         xq_codes = reuse.tile([P, J], U32, name="xq_codes", align_bytes=64, offset=4 * J)
         xq_sc = keep.tile([P, J], U8, name="xq_sc", align_bytes=64)
@@ -119,15 +118,20 @@ def tile_list_tiert_gate_kernel(
             return x_raw[c // 2][:, :, inner : inner + CHUNK].rearrange("p i (g e) -> p g i e", e=run)
 
         def round_x(c):
-            xq_in[c] = ring.tile([P, CHUNK, PACK], BF16, name="xq_in", align_bytes=64)
-            nc.scalar.copy(out=xq_in[c][:].rearrange("p (g e) i -> p g i e", e=4), in_=x_chunk(c, 4))
+            nc.scalar.copy(out=xq_in[:, cols_of(c % 2), :].rearrange("p (g e) i -> p g i e", e=2), in_=x_chunk(c, 2))
 
-        def quantize_x(c):
+        def quantize_x(first, count):
+            cols = slice(first * CHUNK, (first + count) * CHUNK)
+            inner = (first % 2) * CHUNK
             nc.vector.quantize_mx(
-                out=xq_codes[:, cols_of(c)].bitcast(FP8X4),
-                scales=xq_sc[:, cols_of(c)],
-                in_=xq_in[c][:].rearrange("p j i -> p (j i)"),
+                out=xq_codes[:, cols].bitcast(FP8X4),
+                scales=xq_sc[:, cols],
+                in_=xq_in[:, inner : inner + count * CHUNK, :].rearrange("p j i -> p (j i)"),
             )
+            for c in range(first, first + count):
+                decode(c)
+
+        def decode(c):
             bank = psum.tile([P, PACK, CHUNK], F32, name="bank")
             decoded[c] = bank
             for i in range(PACK):
@@ -210,15 +214,14 @@ def tile_list_tiert_gate_kernel(
         round_x(0)
         round_x(1)
         nc.vector.tensor_copy(out=v_sc[:], in_=table_sc[:].indirect(offsets[:]))
-        quantize_x(0)
-        quantize_x(1)
+        quantize_x(0, 2)
         round_x(2)
         round_x(3)
         nc.vector.tensor_copy(out=v_codes[:], in_=table[:].indirect(offsets[:]))
         subtract(0)
-        quantize_x(2)
+        quantize_x(2, 1)
         subtract(1)
-        quantize_x(3)
+        quantize_x(3, 1)
         subtract(2)
         quantize_rest(0, HALF)
         quantize_rest(HALF, EARLY)

@@ -168,10 +168,9 @@ def tile_list_tiert_gate_kernel(
             wx_codes = wx[h][:, inner * P : (inner + 1) * P].bitcast(FP8X4)
             wt_codes = wt[:, 2 * t * P : 2 * (t + 1) * P].bitcast(FP4X4)
             step = J if hi - lo == J else CHUNK
-            wide = [slice(lo, hi)] if hi - lo != EARLY else [slice(0, HALF), slice(HALF, EARLY)]
-            passes = [(wx_codes, 4, xq_codes, xq_sc, cols) for cols in wide]
+            passes = [(wx_codes, 4, xq_codes, xq_sc, slice(lo, hi))]
             passes += [(wt_codes, 0, v_codes, v_sc, slice(c0, c0 + step)) for c0 in range(lo, hi, step)]
-            passes += [(wx_codes, 4, xr_codes, xr_sc, cols) for cols in wide]
+            passes += [(wx_codes, 4, xr_codes, xr_sc, slice(lo, hi))]
             for k, (w_codes, first, codes, sc, cols) in enumerate(passes):
                 nc.tensor.matmul_mx(
                     out=acc[:, cols],
@@ -222,18 +221,18 @@ def tile_list_tiert_gate_kernel(
         quantize_x(2, 1)
         subtract(1)
         quantize_x(3, 1)
-        subtract(2)
         quantize_rest(0, HALF)
-        quantize_rest(HALF, EARLY)
+        subtract(2)
         subtract(3)
+        quantize_rest(HALF, EARLY)
         quantize_rest(EARLY, J)
         sum_part(0, 0, HALF)
+        sum_part(1, 0, HALF)
         sum_part(0, HALF, EARLY)
-        sum_part(1, 0, EARLY)
         sum_part(0, EARLY, J)
-        sum_part(1, EARLY, J)
-        gate_part(0, 0, EARLY)
-        gate_part(0, EARLY, J)
+        sum_part(1, HALF, J)
+        gate_part(0, 0, HALF)
+        gate_part(0, HALF, J)
         gate_part(1, 0, J)
         for t in range(2, N_TILES):
             sum_part(t, 0, J)

@@ -30,7 +30,7 @@ TAIL = CHUNK
 
 def load_scale_rows(queue, plane, rows, first):
     for r in range(4):
-        queue.dma_start(out=plane[first + r : P : 32, :].bitcast(I32), in_=rows[r:16:4, :].bitcast(I32))
+        queue.dma_start(out=plane[first + r : P : 32, 0:N].bitcast(I32), in_=rows[r:16:4, :].bitcast(I32))
 
 
 def tile_list_tiert_gate_kernel(
@@ -44,9 +44,9 @@ def tile_list_tiert_gate_kernel(
 
         offsets = keep.tile([P, J // 16], U16, name="offsets")
         table = keep.tile([P, T], U32, name="table", align_bytes=64)
-        table_sc = keep.tile([P, T], U8, name="table_sc", align_bytes=64)
+        table_sc = keep.tile([P, T + 4], U8, name="table_sc", align_bytes=64)
         wt = keep.tile([P, 2 * N], U8, name="wt", align_bytes=64)
-        w_sc = keep.tile([P, N], U8, name="w_sc", align_bytes=64)
+        w_sc = keep.tile([P, N + 4], U8, name="w_sc", align_bytes=64)
         wx = [keep.tile([P, N // 2], U32, name="wx%d" % h, align_bytes=64) for h in range(2)]
         x_raw = [keep.tile([P, PACK, HALF], F32, name="x_raw%d" % h, align_bytes=64) for h in range(2)]
         gates = [keep.tile([P, T], F32, name="gates%d" % t, align_bytes=64) for t in range(N_TILES)]
@@ -212,7 +212,7 @@ def tile_list_tiert_gate_kernel(
 
         round_x(0)
         round_x(1)
-        nc.vector.tensor_copy(out=v_sc[:], in_=table_sc[:].indirect(offsets[:]))
+        nc.vector.tensor_copy(out=v_sc[:], in_=table_sc[:, 0:T].indirect(offsets[:]))
         quantize_x(0, 2)
         round_x(2)
         round_x(3)

@@ -25,7 +25,7 @@ N_TILES = N // P
 STORE_GROUPS = ((0, 4), (4, 2), (6, 1), (7, 1))
 EARLY = 3 * CHUNK
 GATES_AHEAD = 3
-TAIL = CHUNK
+TAIL = 3 * J // 8
 
 
 def load_scale_rows(queue, plane, rows, first):

@@ -25,6 +25,7 @@ N_TILES = N // P
 STORE_GROUPS = ((0, 4), (4, 2), (6, 1), (7, 1))
 EARLY = 3 * CHUNK
 GATES_AHEAD = 3
+WARM_UP = (512, 512, 256)
 TAIL = 3 * J // 8
 
 
@@ -99,6 +100,18 @@ def tile_list_tiert_gate_kernel(
         nc.vector.quantize_mx(
             out=pick_codes[:].bitcast(FP8X4), scales=pick_sc[:], in_=pick[:, 0 : PACK * width]
         )
+
+        warm = psum.tile([P, J], F32, name="bank")
+        for columns in WARM_UP:
+            nc.tensor.matmul_mx(
+                out=warm[:, 0:columns],
+                lhsT=pick_codes[:, 0:P].bitcast(FP8X4),
+                lhsT_scale=pick_sc[:, 0:P],
+                rhs=pick_codes[:, 0:columns].bitcast(FP8X4),
+                rhs_scale=pick_sc[:, 0:columns],
+                start=True,
+                stop=True,
+            )
 
         v_codes = reuse.tile([P, J], U32, name="v_codes", align_bytes=64, offset=0)
         v_sc = reuse.tile([P, J], U8, name="v_sc", align_bytes=64, offset=8 * J)

@@ -22,9 +22,8 @@ CHUNK = 128
 CHUNKS = J // CHUNK
 HALF = J // 2
 N_TILES = N // P
-STORE_GROUPS = ((0, 4), (4, 2), (6, 1), (7, 1))
+STORE_GROUPS = ((0, 3), (3, 2), (5, 1), (6, 1), (7, 1))
 EARLY = 3 * CHUNK
-GATES_AHEAD = 3
 WARM_UP = (512, 512, 256)
 TAIL = 3 * J // 8
 
@@ -48,7 +47,7 @@ def tile_list_tiert_gate_kernel(
         table_sc = keep.tile([P, T + 4], U8, name="table_sc", align_bytes=64)
         wt = keep.tile([P, 2 * N], U8, name="wt", align_bytes=64)
         w_sc = keep.tile([P, N + 4], U8, name="w_sc", align_bytes=64)
-        wx = [keep.tile([P, N // 2], U32, name="wx%d" % h, align_bytes=64) for h in range(2)]
+        wx = keep.tile([P, N], U32, name="wx", align_bytes=64)
         x_raw = [keep.tile([P, PACK, HALF], F32, name="x_raw%d" % h, align_bytes=64) for h in range(2)]
         gates = [keep.tile([P, T], F32, name="gates%d" % t, align_bytes=64) for t in range(N_TILES)]
 
@@ -60,22 +59,16 @@ def tile_list_tiert_gate_kernel(
         def load_gates(t):
             nc.sync.dma_start(out=gates[t][:], in_=gT[t * P : (t + 1) * P, :])
 
-        def load_wx(h):
-            wx_rows = wx_words[0].rearrange("p n i -> p (n i)").bitcast(I32)
-            nc.sync.dma_start(out=wx[h][:].bitcast(I32), in_=wx_rows[:, h * N // 2 : (h + 1) * N // 2])
-
         nc.sync.dma_start(out=x_raw[0][:], in_=x_rows[:, :, 0:HALF])
         nc.sync.dma_start(out=offsets[:], in_=offs)
         load_scale_rows(nc.sync, table_sc, tab_scales[0], 0)
         nc.sync.dma_start(out=table[:].bitcast(I32), in_=tab_words[0].rearrange("p t i -> p (t i)").bitcast(I32))
         nc.sync.dma_start(out=x_raw[1][:], in_=x_rows[:, :, HALF:J])
         load_scale_rows(nc.sync, w_sc, wx_scales[0], 4)
-        load_wx(0)
+        nc.sync.dma_start(out=wx[:].bitcast(I32), in_=wx_words[0].rearrange("p n i -> p (n i)").bitcast(I32))
         nc.sync.dma_start(out=wt[:].bitcast(I32), in_=wt_words[0].bitcast(I32))
         load_scale_rows(nc.sync, w_sc, wt_scales[0], 0)
         for t in range(N_TILES):
-            if t == GATES_AHEAD:
-                load_wx(1)
             load_gates(t)
 
         width = P * PACK
@@ -177,8 +170,7 @@ def tile_list_tiert_gate_kernel(
 
         def project(acc, t, lo, hi):
             n_cols = slice(t * P, (t + 1) * P)
-            h, inner = divmod(t, N_TILES // 2)
-            wx_codes = wx[h][:, inner * P : (inner + 1) * P].bitcast(FP8X4)
+            wx_codes = wx[:, n_cols].bitcast(FP8X4)
             wt_codes = wt[:, 2 * t * P : 2 * (t + 1) * P].bitcast(FP4X4)
             step = J if hi - lo == J else CHUNK
             passes = [(wx_codes, 4, xq_codes, xq_sc, slice(lo, hi))]

@@ -24,7 +24,7 @@ HALF = J // 2
 N_TILES = N // P
 STORE_GROUPS = ((0, 3), (3, 2), (5, 1), (6, 1), (7, 1))
 EARLY = 3 * CHUNK
-WARM_UP = (512, 512, 256)
+WARM_UP = (128, 256, 512, 512)
 TAIL = 3 * J // 8
 
 

@@ -43,13 +43,13 @@ def tile_list_tiert_gate_kernel(
         psum = ctx.enter_context(tc.psum_pool(name="psum", bufs=8))
 
         offsets = keep.tile([P, J // 16], U16, name="offsets")
-        table = keep.tile([P, T], U32, name="table", align_bytes=64)
-        table_sc = keep.tile([P, T + 4], U8, name="table_sc", align_bytes=64)
-        wt = keep.tile([P, 2 * N], U8, name="wt", align_bytes=64)
-        w_sc = keep.tile([P, N + 4], U8, name="w_sc", align_bytes=64)
-        wx = keep.tile([P, N], U32, name="wx", align_bytes=64)
-        x_raw = [keep.tile([P, PACK, HALF], F32, name="x_raw%d" % h, align_bytes=64) for h in range(2)]
-        gates = [keep.tile([P, T], F32, name="gates%d" % t, align_bytes=64) for t in range(N_TILES)]
+        table = keep.tile([P, T], U32, name="table", align_bytes=256)
+        table_sc = keep.tile([P, T + 4], U8, name="table_sc", align_bytes=256)
+        wt = keep.tile([P, 2 * N], U8, name="wt", align_bytes=256)
+        w_sc = keep.tile([P, N + 4], U8, name="w_sc", align_bytes=256)
+        wx = keep.tile([P, N], U32, name="wx", align_bytes=256)
+        x_raw = [keep.tile([P, PACK, HALF], F32, name="x_raw%d" % h, align_bytes=256) for h in range(2)]
+        gates = [keep.tile([P, T], F32, name="gates%d" % t, align_bytes=256) for t in range(N_TILES)]
 
         for plane in (table_sc, w_sc):
             nc.vector.memset(plane[:].bitcast(I32), 0)
@@ -88,8 +88,8 @@ def tile_list_tiert_gate_kernel(
         for i in range(PACK - 1):
             first = last + PACK - 1 - i
             nc.vector.tensor_copy(out=pick[:, i * width : (i + 1) * width], in_=pick[:, first : first + width])
-        pick_codes = keep.tile([P, PACK * P], U32, name="pick_codes", align_bytes=64)
-        pick_sc = keep.tile([P, PACK * P], U8, name="pick_sc", align_bytes=64)
+        pick_codes = keep.tile([P, PACK * P], U32, name="pick_codes", align_bytes=256)
+        pick_sc = keep.tile([P, PACK * P], U8, name="pick_sc", align_bytes=256)
         nc.vector.quantize_mx(
             out=pick_codes[:].bitcast(FP8X4), scales=pick_sc[:], in_=pick[:, 0 : PACK * width]
         )
@@ -108,12 +108,12 @@ def tile_list_tiert_gate_kernel(
 
         v_codes = reuse.tile([P, J], U32, name="v_codes", align_bytes=64, offset=0)
         v_sc = reuse.tile([P, J], U8, name="v_sc", align_bytes=64, offset=8 * J)
-        xq_in = keep.tile([P, HALF, PACK], BF16, name="xq_in", align_bytes=64)
-        xr_in = keep.tile([P, J, PACK], BF16, name="xr_in", align_bytes=64)
+        xq_in = keep.tile([P, HALF, PACK], BF16, name="xq_in", align_bytes=256)
+        xr_in = keep.tile([P, J, PACK], BF16, name="xr_in", align_bytes=256)
         xq_codes = reuse.tile([P, J], U32, name="xq_codes", align_bytes=64, offset=4 * J)
-        xq_sc = keep.tile([P, J], U8, name="xq_sc", align_bytes=64)
-        xr_codes = keep.tile([P, J], U32, name="xr_codes", align_bytes=64)
-        xr_sc = keep.tile([P, J], U8, name="xr_sc", align_bytes=64)
+        xq_sc = keep.tile([P, J], U8, name="xq_sc", align_bytes=256)
+        xr_codes = keep.tile([P, J], U32, name="xr_codes", align_bytes=256)
+        xr_sc = keep.tile([P, J], U8, name="xr_sc", align_bytes=256)
         decoded = {}
 
         def cols_of(c):
@@ -187,10 +187,10 @@ def tile_list_tiert_gate_kernel(
                     stop=(k == len(passes) - 1),
                 )
 
-        sums = [keep.tile([P, J], F32, name="sums%d" % t, align_bytes=64) for t in range(N_TILES)]
+        sums = [keep.tile([P, J], F32, name="sums%d" % t, align_bytes=256) for t in range(N_TILES)]
         gated = {}
         for first, count in STORE_GROUPS:
-            group = keep.tile([P, count, J], F32, name="gated%d" % first, align_bytes=64)
+            group = keep.tile([P, count, J], F32, name="gated%d" % first, align_bytes=256)
             for k in range(count):
                 gated[first + k] = (group, first, count)
 

@@ -168,24 +168,35 @@ def tile_list_tiert_gate_kernel(
                 in_=xr_in[:, cols, :].rearrange("p j i -> p (j i)"),
             )
 
-        def project(acc, t, lo, hi):
-            n_cols = slice(t * P, (t + 1) * P)
-            wx_codes = wx[:, n_cols].bitcast(FP8X4)
+        banks = {}
+
+        def one_pass(t, w_codes, first, codes, sc, lo, hi, c0, c1, start, stop):
+            if start:
+                banks[t, lo] = psum.tile([P, J], F32, name="bank")
+            nc.tensor.matmul_mx(
+                out=banks[t, lo][:, c0:c1],
+                lhsT=w_codes,
+                lhsT_scale=w_sc[first:P, t * P : (t + 1) * P],
+                rhs=codes[:, c0:c1].bitcast(FP8X4),
+                rhs_scale=sc[:, c0:c1],
+                start=start,
+                stop=stop,
+            )
+
+        def first_tier(t, lo, hi):
+            wx_codes = wx[:, t * P : (t + 1) * P].bitcast(FP8X4)
+            one_pass(t, wx_codes, 4, xq_codes, xq_sc, lo, hi, lo, hi, True, False)
+
+        def table_part(t, lo, hi):
             wt_codes = wt[:, 2 * t * P : 2 * (t + 1) * P].bitcast(FP4X4)
             step = J if hi - lo == J else CHUNK
-            passes = [(wx_codes, 4, xq_codes, xq_sc, slice(lo, hi))]
-            passes += [(wt_codes, 0, v_codes, v_sc, slice(c0, c0 + step)) for c0 in range(lo, hi, step)]
-            passes += [(wx_codes, 4, xr_codes, xr_sc, slice(lo, hi))]
-            for k, (w_codes, first, codes, sc, cols) in enumerate(passes):
-                nc.tensor.matmul_mx(
-                    out=acc[:, cols],
-                    lhsT=w_codes,
-                    lhsT_scale=w_sc[first:P, n_cols],
-                    rhs=codes[:, cols].bitcast(FP8X4),
-                    rhs_scale=sc[:, cols],
-                    start=(k == 0),
-                    stop=(k == len(passes) - 1),
-                )
+            for c0 in range(lo, hi, step):
+                one_pass(t, wt_codes, 0, v_codes, v_sc, lo, hi, c0, c0 + step, False, False)
+
+        def second_tier(t, lo, hi):
+            wx_codes = wx[:, t * P : (t + 1) * P].bitcast(FP8X4)
+            one_pass(t, wx_codes, 4, xr_codes, xr_sc, lo, hi, lo, hi, False, True)
+            nc.scalar.copy(out=sums[t][:, lo:hi], in_=banks[t, lo][:, lo:hi])
 
         sums = [keep.tile([P, J], F32, name="sums%d" % t, align_bytes=256) for t in range(N_TILES)]
         gated = {}
@@ -193,13 +204,6 @@ def tile_list_tiert_gate_kernel(
             group = keep.tile([P, count, J], F32, name="gated%d" % first, align_bytes=256)
             for k in range(count):
                 gated[first + k] = (group, first, count)
-
-        def sum_part(t, *edges):
-            acc = psum.tile([P, J], F32, name="bank")
-            lo, hi = edges[0], edges[-1]
-            for k in range(len(edges) - 1):
-                project(acc, t, edges[k], edges[k + 1])
-            nc.scalar.copy(out=sums[t][:, lo:hi], in_=acc[:, lo:hi])
 
         def gate_part(t, lo, hi):
             nc.vector.tensor_tensor(
@@ -231,16 +235,22 @@ def tile_list_tiert_gate_kernel(
         subtract(3)
         quantize_rest(HALF, EARLY)
         quantize_rest(EARLY, J)
-        sum_part(0, 0, HALF)
-        sum_part(1, 0, HALF)
-        sum_part(0, HALF, EARLY)
-        sum_part(0, EARLY, J)
-        sum_part(1, HALF, J)
+        first_tier(0, 0, HALF)
+        first_tier(1, 0, HALF)
+        for t in range(2):
+            table_part(t, 0, HALF)
+            second_tier(t, 0, HALF)
+        for part in ((0, HALF, EARLY), (0, EARLY, J), (1, HALF, J)):
+            first_tier(*part)
+            table_part(*part)
+            second_tier(*part)
         gate_part(0, 0, HALF)
         gate_part(0, HALF, J)
         gate_part(1, 0, J)
         for t in range(2, N_TILES):
-            sum_part(t, 0, J)
+            first_tier(t, 0, J)
+            table_part(t, 0, J)
+            second_tier(t, 0, J)
             edges = (0, J - TAIL, J) if t == N_TILES - 1 else (0, J)
             for k in range(len(edges) - 1):
                 gate_part(t, edges[k], edges[k + 1])

@@ -240,10 +240,14 @@ def tile_list_tiert_gate_kernel(
         for t in range(2):
             table_part(t, 0, HALF)
             second_tier(t, 0, HALF)
-        for part in ((0, HALF, EARLY), (0, EARLY, J), (1, HALF, J)):
-            first_tier(*part)
-            table_part(*part)
-            second_tier(*part)
+        for lo in (HALF, EARLY):
+            first_tier(0, lo, lo + CHUNK)
+            table_part(0, lo, lo + CHUNK)
+        for lo in (HALF, EARLY):
+            second_tier(0, lo, lo + CHUNK)
+        first_tier(1, HALF, J)
+        table_part(1, HALF, J)
+        second_tier(1, HALF, J)
         gate_part(0, 0, HALF)
         gate_part(0, HALF, J)
         gate_part(1, 0, J)

@@ -19,18 +19,19 @@ SUBTRACT = mybir.AluOpType.subtract
 P = 128
 PACK = 4
 CHUNK = 128
-CHUNKS = J // CHUNK
 HALF = J // 2
 N_TILES = N // P
-STORE_GROUPS = ((0, 3), (3, 2), (5, 1), (6, 1), (7, 1))
-EARLY = 3 * CHUNK
+X_LOADS = ((0, 1), (1, 1), (2, 2))
+STORE_GROUPS = tuple((t, 1) for t in range(N_TILES))
 WARM_UP = (128, 256, 512, 512)
 TAIL = 3 * J // 8
-
-
-def load_scale_rows(queue, plane, rows, first):
-    for r in range(4):
-        queue.dma_start(out=plane[first + r : P : 32, 0:N].bitcast(I32), in_=rows[r:16:4, :].bitcast(I32))
+BLOCKS = 16
+GATE_BYTES = 4 * T
+KB = 1024
+GATE_AT = (4, 8, 13, 21, 25, 29, 33, 37)
+X_AT = (11.5, 18, 31)
+EARLY = N // 2
+WT_COL, WX_COL, V_COL = 0, N, 2 * N
 
 
 def tile_list_tiert_gate_kernel(
@@ -39,42 +40,70 @@ def tile_list_tiert_gate_kernel(
     nc = tc.nc
     with ExitStack() as ctx:
         keep = ctx.enter_context(tc.tile_pool(name="keep", bufs=1))
-        reuse = ctx.enter_context(tc.tile_pool(name="reuse", bufs=1))
+        stream = ctx.enter_context(tc.tile_pool(name="stream", bufs=1))
         psum = ctx.enter_context(tc.psum_pool(name="psum", bufs=8))
 
         offsets = keep.tile([P, J // 16], U16, name="offsets")
-        table = keep.tile([P, T], U32, name="table", align_bytes=256)
+        table = stream.tile([P, T], U32, name="table", align_bytes=256, offset=23 * KB)
         table_sc = keep.tile([P, T + 4], U8, name="table_sc", align_bytes=256)
-        wt = keep.tile([P, 2 * N], U8, name="wt", align_bytes=256)
-        w_sc = keep.tile([P, N + 4], U8, name="w_sc", align_bytes=256)
-        wx = keep.tile([P, N], U32, name="wx", align_bytes=256)
-        x_raw = [keep.tile([P, PACK, HALF], F32, name="x_raw%d" % h, align_bytes=256) for h in range(2)]
-        gates = [keep.tile([P, T], F32, name="gates%d" % t, align_bytes=256) for t in range(N_TILES)]
+        wt = (
+            keep.tile([P, 2 * EARLY], U8, name="wt_early", align_bytes=256),
+            stream.tile([P, 2 * EARLY], U8, name="wt_late", align_bytes=256, offset=12 * KB),
+        )
+        planes = keep.tile([P, 2 * N + J + 4], U8, name="planes", align_bytes=256)
+        wx = (
+            keep.tile([P, EARLY], U32, name="wx_early", align_bytes=256),
+            stream.tile([P, EARLY], U32, name="wx_late", align_bytes=256, offset=17 * KB),
+        )
+        x_raw = [
+            stream.tile(
+                [P, PACK, count * CHUNK],
+                F32,
+                name="x_raw%d" % first,
+                align_bytes=256,
+                offset=int(X_AT[k] * KB),
+            )
+            for k, (first, count) in enumerate(X_LOADS)
+        ]
+        picked_sc = stream.tile([P, J], U8, name="picked_sc", align_bytes=256, offset=GATE_BYTES)
+        gates = [
+            stream.tile([P, T], F32, name="gates%d" % t, align_bytes=256, offset=GATE_AT[t] * KB) for t in range(N_TILES)
+        ]
 
-        for plane in (table_sc, w_sc):
+        for plane in (table_sc, planes):
             nc.vector.memset(plane[:].bitcast(I32), 0)
 
         x_rows = x.rearrange("(p i) j -> p i j", i=PACK)
 
+        def load_x(k):
+            first, count = X_LOADS[k]
+            nc.sync.dma_start(out=x_raw[k][:], in_=x_rows[:, :, first * CHUNK : (first + count) * CHUNK])
+
+        def load_words(tile, words):
+            nc.sync.dma_start(out=tile[:].bitcast(I32), in_=words.bitcast(I32))
+
+        def load_scale_rows(plane, rows, column):
+            nc.sync.dma_start(out=plane[0:BLOCKS, column : column + N].bitcast(I32), in_=rows.bitcast(I32))
+
         def load_gates(t):
             nc.sync.dma_start(out=gates[t][:], in_=gT[t * P : (t + 1) * P, :])
 
-        nc.sync.dma_start(out=x_raw[0][:], in_=x_rows[:, :, 0:HALF])
+        load_x(0)
         nc.sync.dma_start(out=offsets[:], in_=offs)
-        load_scale_rows(nc.sync, table_sc, tab_scales[0], 0)
-        nc.sync.dma_start(out=table[:].bitcast(I32), in_=tab_words[0].rearrange("p t i -> p (t i)").bitcast(I32))
-        nc.sync.dma_start(out=x_raw[1][:], in_=x_rows[:, :, HALF:J])
-        load_scale_rows(nc.sync, w_sc, wx_scales[0], 4)
-        nc.sync.dma_start(out=wx[:].bitcast(I32), in_=wx_words[0].rearrange("p n i -> p (n i)").bitcast(I32))
-        nc.sync.dma_start(out=wt[:].bitcast(I32), in_=wt_words[0].bitcast(I32))
-        load_scale_rows(nc.sync, w_sc, wt_scales[0], 0)
-        for t in range(N_TILES):
-            load_gates(t)
+        load_scale_rows(table_sc, tab_scales[0], 0)
+        load_x(1)
+        load_x(2)
+        load_scale_rows(planes, wx_scales[0], WX_COL)
+        load_scale_rows(planes, wt_scales[0], WT_COL)
+        load_words(table, tab_words[0].rearrange("p t i -> p (t i)"))
+        wx_rows = wx_words[0].rearrange("p n i -> p (n i)")
+        load_words(wx[0], wx_rows[:, 0 : PACK * EARLY])
+        load_words(wt[0], wt_words[0][:, 0 : 2 * EARLY])
 
         width = P * PACK
-        pick = reuse.tile([P, PACK * width + 32], BF16, name="pick", align_bytes=64, offset=0)
-        last = (PACK - 1) * width
-        source = pick[:, last : last + width + 32]
+        pick_lo = stream.tile([P, 2 * width], BF16, name="pick_lo", align_bytes=256, offset=GATE_BYTES - 1024)
+        pick_hi = keep.tile([P, 2 * width + 32], BF16, name="pick_hi", align_bytes=256)
+        source = pick_hi[:, width : 2 * width + 32]
         nc.gpsimd.memset(source.bitcast(I32), 0)
         nc.gpsimd.affine_select(
             out=source.bitcast(F32),
@@ -85,14 +114,18 @@ def tile_list_tiert_gate_kernel(
             pattern=[[-1, (width + 32) // 2]],
             channel_multiplier=2,
         )
+        targets = (pick_lo[:, 0:width], pick_lo[:, width : 2 * width], pick_hi[:, 0:width])
         for i in range(PACK - 1):
-            first = last + PACK - 1 - i
-            nc.vector.tensor_copy(out=pick[:, i * width : (i + 1) * width], in_=pick[:, first : first + width])
+            first = PACK - 1 - i
+            nc.vector.tensor_copy(out=targets[i], in_=source[:, first : first + width])
         pick_codes = keep.tile([P, PACK * P], U32, name="pick_codes", align_bytes=256)
         pick_sc = keep.tile([P, PACK * P], U8, name="pick_sc", align_bytes=256)
-        nc.vector.quantize_mx(
-            out=pick_codes[:].bitcast(FP8X4), scales=pick_sc[:], in_=pick[:, 0 : PACK * width]
-        )
+        for h, half in enumerate((pick_lo, pick_hi)):
+            nc.vector.quantize_mx(
+                out=pick_codes[:, 2 * h * P : 2 * (h + 1) * P].bitcast(FP8X4),
+                scales=pick_sc[:, 2 * h * P : 2 * (h + 1) * P],
+                in_=half[:, 0 : 2 * width],
+            )
 
         warm = psum.tile([P, J], F32, name="bank")
         for columns in WARM_UP:
@@ -106,11 +139,14 @@ def tile_list_tiert_gate_kernel(
                 stop=True,
             )
 
-        v_codes = reuse.tile([P, J], U32, name="v_codes", align_bytes=64, offset=0)
-        v_sc = reuse.tile([P, J], U8, name="v_sc", align_bytes=64, offset=8 * J)
-        xq_in = keep.tile([P, HALF, PACK], BF16, name="xq_in", align_bytes=256)
-        xr_in = keep.tile([P, J, PACK], BF16, name="xr_in", align_bytes=256)
-        xq_codes = reuse.tile([P, J], U32, name="xq_codes", align_bytes=64, offset=4 * J)
+        v_codes = stream.tile([P, J], U32, name="v_codes", align_bytes=256, offset=19 * KB)
+        v_sc = planes[:, V_COL : V_COL + J]
+        xq_lo = keep.tile([P, CHUNK, PACK], BF16, name="xq_lo", align_bytes=256)
+        xq_mid = stream.tile([P, CHUNK, PACK], BF16, name="xq_mid", align_bytes=256, offset=0)
+        xq_hi = stream.tile([P, HALF, PACK], BF16, name="xq_hi", align_bytes=256, offset=0)
+        xq_in = (xq_lo[:], xq_mid[:], xq_hi[:, 0:CHUNK, :], xq_hi[:, CHUNK:HALF, :])
+        xr_in = stream.tile([P, J, PACK], BF16, name="xr_in", align_bytes=256, offset=37 * KB)
+        xq_codes = stream.tile([P, J], U32, name="xq_codes", align_bytes=256, offset=4 * J)
         xq_sc = keep.tile([P, J], U8, name="xq_sc", align_bytes=256)
         xr_codes = keep.tile([P, J], U32, name="xr_codes", align_bytes=256)
         xr_sc = keep.tile([P, J], U8, name="xr_sc", align_bytes=256)
@@ -119,23 +155,21 @@ def tile_list_tiert_gate_kernel(
         def cols_of(c):
             return slice(c * CHUNK, (c + 1) * CHUNK)
 
-        def x_chunk(c, run):
-            inner = (c % 2) * CHUNK
-            return x_raw[c // 2][:, :, inner : inner + CHUNK].rearrange("p i (g e) -> p g i e", e=run)
+        def x_chunk(c):
+            for k, (first, count) in enumerate(X_LOADS):
+                if first <= c < first + count:
+                    return x_raw[k][:, :, cols_of(c - first)].rearrange("p i (g e) -> p g i e", e=2)
 
         def round_x(c):
-            nc.scalar.copy(out=xq_in[:, cols_of(c % 2), :].rearrange("p (g e) i -> p g i e", e=2), in_=x_chunk(c, 2))
+            nc.scalar.copy(out=xq_in[c].rearrange("p (g e) i -> p g i e", e=2), in_=x_chunk(c))
 
-        def quantize_x(first, count):
-            cols = slice(first * CHUNK, (first + count) * CHUNK)
-            inner = (first % 2) * CHUNK
+        def quantize_x(c):
             nc.vector.quantize_mx(
-                out=xq_codes[:, cols].bitcast(FP8X4),
-                scales=xq_sc[:, cols],
-                in_=xq_in[:, inner : inner + count * CHUNK, :].rearrange("p j i -> p (j i)"),
+                out=xq_codes[:, cols_of(c)].bitcast(FP8X4),
+                scales=xq_sc[:, cols_of(c)],
+                in_=xq_in[c].rearrange("p j i -> p (j i)"),
             )
-            for c in range(first, first + count):
-                decode(c)
+            decode(c)
 
         def decode(c):
             bank = psum.tile([P, PACK, CHUNK], F32, name="bank")
@@ -155,48 +189,63 @@ def tile_list_tiert_gate_kernel(
         def subtract(c):
             nc.vector.tensor_tensor(
                 out=xr_in[:, cols_of(c), :].rearrange("p (g e) i -> p g i e", e=2),
-                in0=x_chunk(c, 2),
+                in0=x_chunk(c),
                 in1=decoded[c][:].rearrange("p i (g e) -> p g i e", e=2),
                 op=SUBTRACT,
             )
 
-        def quantize_rest(lo, hi):
-            cols = slice(lo, hi)
+        def quantize_rest(first, count):
+            cols = slice(first * CHUNK, (first + count) * CHUNK)
             nc.vector.quantize_mx(
                 out=xr_codes[:, cols].bitcast(FP8X4),
                 scales=xr_sc[:, cols],
                 in_=xr_in[:, cols, :].rearrange("p j i -> p (j i)"),
             )
 
+        def gather_scales(lo, hi):
+            nc.vector.tensor_copy(out=picked_sc[:, lo:hi], in_=table_sc[:, 0:T].indirect(offsets[:, lo // 16 : hi // 16]))
+
+        def spread_scale_rows():
+            nc.vector.tensor_copy(out=planes[0:32, V_COL : V_COL + J].bitcast(I32), in_=picked_sc[0:32, :].bitcast(I32))
+            for q in range(1, 4):
+                nc.sync.dma_start(
+                    out=planes[32 * q : 32 * q + 4, 0 : V_COL + J].bitcast(I32),
+                    in_=planes[4 * q : 4 * q + 4, 0 : V_COL + J].bitcast(I32),
+                )
+
+        def gather_words(lo, hi):
+            nc.vector.tensor_copy(out=v_codes[:, lo:hi], in_=table[:].indirect(offsets[:, lo // 16 : hi // 16]))
+
         banks = {}
 
-        def one_pass(t, w_codes, first, codes, sc, lo, hi, c0, c1, start, stop):
+        def one_pass(t, w_codes, first, codes, sc, lo, c0, c1, start, stop):
             if start:
                 banks[t, lo] = psum.tile([P, J], F32, name="bank")
             nc.tensor.matmul_mx(
                 out=banks[t, lo][:, c0:c1],
                 lhsT=w_codes,
-                lhsT_scale=w_sc[first:P, t * P : (t + 1) * P],
+                lhsT_scale=planes[:, first + t * P : first + (t + 1) * P],
                 rhs=codes[:, c0:c1].bitcast(FP8X4),
                 rhs_scale=sc[:, c0:c1],
                 start=start,
                 stop=stop,
             )
+            if stop:
+                nc.scalar.copy(out=sums[t][:, lo:c1], in_=banks[t, lo][:, lo:c1])
 
         def first_tier(t, lo, hi):
-            wx_codes = wx[:, t * P : (t + 1) * P].bitcast(FP8X4)
-            one_pass(t, wx_codes, 4, xq_codes, xq_sc, lo, hi, lo, hi, True, False)
+            wx_codes = wx[t // 4][:, (t % 4) * P : (t % 4 + 1) * P].bitcast(FP8X4)
+            one_pass(t, wx_codes, WX_COL, xq_codes, xq_sc, lo, lo, hi, True, False)
 
-        def table_part(t, lo, hi):
-            wt_codes = wt[:, 2 * t * P : 2 * (t + 1) * P].bitcast(FP4X4)
+        def table_part(t, lo, hi, stop=False):
+            wt_codes = wt[t // 4][:, 2 * (t % 4) * P : 2 * (t % 4 + 1) * P].bitcast(FP4X4)
             step = J if hi - lo == J else CHUNK
             for c0 in range(lo, hi, step):
-                one_pass(t, wt_codes, 0, v_codes, v_sc, lo, hi, c0, c0 + step, False, False)
+                one_pass(t, wt_codes, WT_COL, v_codes, v_sc, lo, c0, c0 + step, False, stop and c0 + step == hi)
 
-        def second_tier(t, lo, hi):
-            wx_codes = wx[:, t * P : (t + 1) * P].bitcast(FP8X4)
-            one_pass(t, wx_codes, 4, xr_codes, xr_sc, lo, hi, lo, hi, False, True)
-            nc.scalar.copy(out=sums[t][:, lo:hi], in_=banks[t, lo][:, lo:hi])
+        def second_tier(t, lo, hi, stop=True):
+            wx_codes = wx[t // 4][:, (t % 4) * P : (t % 4 + 1) * P].bitcast(FP8X4)
+            one_pass(t, wx_codes, WX_COL, xr_codes, xr_sc, lo, lo, hi, False, stop)
 
         sums = [keep.tile([P, J], F32, name="sums%d" % t, align_bytes=256) for t in range(N_TILES)]
         gated = {}
@@ -221,36 +270,53 @@ def tile_list_tiert_gate_kernel(
 
         round_x(0)
         round_x(1)
-        nc.vector.tensor_copy(out=v_sc[:], in_=table_sc[:, 0:T].indirect(offsets[:]))
-        quantize_x(0, 2)
+        gather_scales(0, HALF)
+        quantize_x(0)
+        gather_scales(HALF, J)
+        quantize_x(1)
+        spread_scale_rows()
+        load_gates(0)
         round_x(2)
         round_x(3)
-        nc.vector.tensor_copy(out=v_codes[:], in_=table[:].indirect(offsets[:]))
         subtract(0)
-        quantize_x(2, 1)
+        load_gates(1)
+        load_gates(2)
+        load_words(wt[1], wt_words[0][:, 2 * EARLY : 2 * N])
         subtract(1)
-        quantize_x(3, 1)
-        quantize_rest(0, HALF)
+        load_words(wx[1], wx_rows[:, PACK * EARLY : PACK * N])
+        quantize_x(2)
+        quantize_x(3)
+        gather_words(0, J)
+        load_gates(3)
+        load_gates(4)
+        quantize_rest(0, 2)
         subtract(2)
         subtract(3)
-        quantize_rest(HALF, EARLY)
-        quantize_rest(EARLY, J)
+        load_gates(5)
+        load_gates(6)
+        quantize_rest(2, 1)
+        quantize_rest(3, 1)
+        load_gates(7)
         first_tier(0, 0, HALF)
         first_tier(1, 0, HALF)
         for t in range(2):
-            table_part(t, 0, HALF)
-            second_tier(t, 0, HALF)
-        for lo in (HALF, EARLY):
-            first_tier(0, lo, lo + CHUNK)
-            table_part(0, lo, lo + CHUNK)
-        for lo in (HALF, EARLY):
-            second_tier(0, lo, lo + CHUNK)
+            second_tier(t, 0, HALF, stop=False)
+        for t in range(2):
+            table_part(t, 0, HALF, stop=True)
+        for c in (2, 3):
+            first_tier(0, c * CHUNK, (c + 1) * CHUNK)
+            table_part(0, c * CHUNK, (c + 1) * CHUNK)
+        for c in (2, 3):
+            second_tier(0, c * CHUNK, (c + 1) * CHUNK)
         first_tier(1, HALF, J)
         table_part(1, HALF, J)
         second_tier(1, HALF, J)
         gate_part(0, 0, HALF)
-        gate_part(0, HALF, J)
+        gate_part(0, HALF, 3 * CHUNK)
+        gate_part(0, 3 * CHUNK, J)
+        store(0, 0, J)
         gate_part(1, 0, J)
+        store(1, 0, J)
         for t in range(2, N_TILES):
             first_tier(t, 0, J)
             table_part(t, 0, J)

@@ -28,8 +28,8 @@ TAIL = 3 * J // 8
 BLOCKS = 16
 GATE_BYTES = 4 * T
 KB = 1024
-GATE_AT = (4, 8, 13, 21, 25, 29, 33, 37)
-X_AT = (11.5, 18, 31)
+GATE_AT = (4, 8, 13, 19, 23, 27, 31, 35)
+X_AT = (18, 26, 33)
 EARLY = N // 2
 WT_COL, WX_COL, V_COL = 0, N, 2 * N
 
@@ -44,8 +44,8 @@ def tile_list_tiert_gate_kernel(
         psum = ctx.enter_context(tc.psum_pool(name="psum", bufs=8))
 
         offsets = keep.tile([P, J // 16], U16, name="offsets")
-        table = stream.tile([P, T], U32, name="table", align_bytes=256, offset=23 * KB)
-        table_sc = keep.tile([P, T + 4], U8, name="table_sc", align_bytes=256)
+        table = stream.tile([P, T], U32, name="table", align_bytes=256, offset=21 * KB // 2)
+        table_sc = stream.tile([P, T + 4], U8, name="table_sc", align_bytes=256, offset=0)
         wt = (
             keep.tile([P, 2 * EARLY], U8, name="wt_early", align_bytes=256),
             stream.tile([P, 2 * EARLY], U8, name="wt_late", align_bytes=256, offset=12 * KB),
@@ -61,7 +61,7 @@ def tile_list_tiert_gate_kernel(
                 F32,
                 name="x_raw%d" % first,
                 align_bytes=256,
-                offset=int(X_AT[k] * KB),
+                offset=X_AT[k] * KB,
             )
             for k, (first, count) in enumerate(X_LOADS)
         ]
@@ -92,18 +92,18 @@ def tile_list_tiert_gate_kernel(
         nc.sync.dma_start(out=offsets[:], in_=offs)
         load_scale_rows(table_sc, tab_scales[0], 0)
         load_x(1)
-        load_x(2)
+        load_words(table, tab_words[0].rearrange("p t i -> p (t i)"))
         load_scale_rows(planes, wx_scales[0], WX_COL)
         load_scale_rows(planes, wt_scales[0], WT_COL)
-        load_words(table, tab_words[0].rearrange("p t i -> p (t i)"))
+        load_x(2)
         wx_rows = wx_words[0].rearrange("p n i -> p (n i)")
         load_words(wx[0], wx_rows[:, 0 : PACK * EARLY])
         load_words(wt[0], wt_words[0][:, 0 : 2 * EARLY])
 
         width = P * PACK
-        pick_lo = stream.tile([P, 2 * width], BF16, name="pick_lo", align_bytes=256, offset=GATE_BYTES - 1024)
-        pick_hi = keep.tile([P, 2 * width + 32], BF16, name="pick_hi", align_bytes=256)
-        source = pick_hi[:, width : 2 * width + 32]
+        pick = stream.tile([P, PACK * width + 32], BF16, name="pick", align_bytes=256, offset=GATE_BYTES - 1024)
+        last = (PACK - 1) * width
+        source = pick[:, last : last + width + 32]
         nc.gpsimd.memset(source.bitcast(I32), 0)
         nc.gpsimd.affine_select(
             out=source.bitcast(F32),
@@ -114,18 +114,12 @@ def tile_list_tiert_gate_kernel(
             pattern=[[-1, (width + 32) // 2]],
             channel_multiplier=2,
         )
-        targets = (pick_lo[:, 0:width], pick_lo[:, width : 2 * width], pick_hi[:, 0:width])
         for i in range(PACK - 1):
             first = PACK - 1 - i
-            nc.vector.tensor_copy(out=targets[i], in_=source[:, first : first + width])
+            nc.vector.tensor_copy(out=pick[:, i * width : (i + 1) * width], in_=source[:, first : first + width])
         pick_codes = keep.tile([P, PACK * P], U32, name="pick_codes", align_bytes=256)
         pick_sc = keep.tile([P, PACK * P], U8, name="pick_sc", align_bytes=256)
-        for h, half in enumerate((pick_lo, pick_hi)):
-            nc.vector.quantize_mx(
-                out=pick_codes[:, 2 * h * P : 2 * (h + 1) * P].bitcast(FP8X4),
-                scales=pick_sc[:, 2 * h * P : 2 * (h + 1) * P],
-                in_=half[:, 0 : 2 * width],
-            )
+        nc.vector.quantize_mx(out=pick_codes[:].bitcast(FP8X4), scales=pick_sc[:], in_=pick[:, 0 : PACK * width])
 
         warm = psum.tile([P, J], F32, name="bank")
         for columns in WARM_UP:
@@ -139,13 +133,10 @@ def tile_list_tiert_gate_kernel(
                 stop=True,
             )
 
-        v_codes = stream.tile([P, J], U32, name="v_codes", align_bytes=256, offset=19 * KB)
+        v_codes = stream.tile([P, J], U32, name="v_codes", align_bytes=256, offset=0)
         v_sc = planes[:, V_COL : V_COL + J]
-        xq_lo = keep.tile([P, CHUNK, PACK], BF16, name="xq_lo", align_bytes=256)
-        xq_mid = stream.tile([P, CHUNK, PACK], BF16, name="xq_mid", align_bytes=256, offset=0)
-        xq_hi = stream.tile([P, HALF, PACK], BF16, name="xq_hi", align_bytes=256, offset=0)
-        xq_in = (xq_lo[:], xq_mid[:], xq_hi[:, 0:CHUNK, :], xq_hi[:, CHUNK:HALF, :])
-        xr_in = stream.tile([P, J, PACK], BF16, name="xr_in", align_bytes=256, offset=37 * KB)
+        xq_in = keep.tile([P, HALF, PACK], BF16, name="xq_in", align_bytes=256)
+        xr_in = keep.tile([P, J, PACK], BF16, name="xr_in", align_bytes=256)
         xq_codes = stream.tile([P, J], U32, name="xq_codes", align_bytes=256, offset=4 * J)
         xq_sc = keep.tile([P, J], U8, name="xq_sc", align_bytes=256)
         xr_codes = keep.tile([P, J], U32, name="xr_codes", align_bytes=256)
@@ -161,15 +152,18 @@ def tile_list_tiert_gate_kernel(
                     return x_raw[k][:, :, cols_of(c - first)].rearrange("p i (g e) -> p g i e", e=2)
 
         def round_x(c):
-            nc.scalar.copy(out=xq_in[c].rearrange("p (g e) i -> p g i e", e=2), in_=x_chunk(c))
+            nc.scalar.copy(out=xq_in[:, cols_of(c % 2), :].rearrange("p (g e) i -> p g i e", e=2), in_=x_chunk(c))
 
-        def quantize_x(c):
+        def quantize_x(first, count):
+            cols = slice(first * CHUNK, (first + count) * CHUNK)
+            inner = (first % 2) * CHUNK
             nc.vector.quantize_mx(
-                out=xq_codes[:, cols_of(c)].bitcast(FP8X4),
-                scales=xq_sc[:, cols_of(c)],
-                in_=xq_in[c].rearrange("p j i -> p (j i)"),
+                out=xq_codes[:, cols].bitcast(FP8X4),
+                scales=xq_sc[:, cols],
+                in_=xq_in[:, inner : inner + count * CHUNK, :].rearrange("p j i -> p (j i)"),
             )
-            decode(c)
+            for c in range(first, first + count):
+                decode(c)
 
         def decode(c):
             bank = psum.tile([P, PACK, CHUNK], F32, name="bank")
@@ -270,50 +264,44 @@ def tile_list_tiert_gate_kernel(
 
         round_x(0)
         round_x(1)
-        gather_scales(0, HALF)
-        quantize_x(0)
-        gather_scales(HALF, J)
-        quantize_x(1)
+        gather_scales(0, J)
+        quantize_x(0, 2)
         spread_scale_rows()
         load_gates(0)
         round_x(2)
         round_x(3)
-        subtract(0)
+        gather_words(0, J)
         load_gates(1)
         load_gates(2)
         load_words(wt[1], wt_words[0][:, 2 * EARLY : 2 * N])
-        subtract(1)
+        subtract(0)
         load_words(wx[1], wx_rows[:, PACK * EARLY : PACK * N])
-        quantize_x(2)
-        quantize_x(3)
-        gather_words(0, J)
         load_gates(3)
+        quantize_x(2, 1)
+        subtract(1)
         load_gates(4)
+        load_gates(5)
+        quantize_x(3, 1)
         quantize_rest(0, 2)
         subtract(2)
         subtract(3)
-        load_gates(5)
         load_gates(6)
+        load_gates(7)
         quantize_rest(2, 1)
         quantize_rest(3, 1)
-        load_gates(7)
-        first_tier(0, 0, HALF)
-        first_tier(1, 0, HALF)
-        for t in range(2):
-            second_tier(t, 0, HALF, stop=False)
-        for t in range(2):
-            table_part(t, 0, HALF, stop=True)
-        for c in (2, 3):
-            first_tier(0, c * CHUNK, (c + 1) * CHUNK)
-            table_part(0, c * CHUNK, (c + 1) * CHUNK)
-        for c in (2, 3):
-            second_tier(0, c * CHUNK, (c + 1) * CHUNK)
-        first_tier(1, HALF, J)
-        table_part(1, HALF, J)
-        second_tier(1, HALF, J)
+        parts = ((0, 0, HALF), (1, 0, HALF), (0, HALF, 3 * CHUNK), (0, 3 * CHUNK, J), (1, HALF, J))
+        for part in parts[:2]:
+            first_tier(*part)
+            table_part(*part)
+        for part in parts[:2]:
+            second_tier(*part)
+        for part in parts[2:]:
+            first_tier(*part)
+            table_part(*part)
+        for part in parts[2:]:
+            second_tier(*part)
         gate_part(0, 0, HALF)
-        gate_part(0, HALF, 3 * CHUNK)
-        gate_part(0, 3 * CHUNK, J)
+        gate_part(0, HALF, J)
         store(0, 0, J)
         gate_part(1, 0, J)
         store(1, 0, J)

@@ -21,15 +21,15 @@ PACK = 4
 CHUNK = 128
 HALF = J // 2
 N_TILES = N // P
-X_LOADS = ((0, 1), (1, 1), (2, 2))
-STORE_GROUPS = tuple((t, 1) for t in range(N_TILES))
+X_LOADS = ((0, 1), (1, 1), (2, 1), (3, 1))
+STORE_GROUPS = ((0, 2),) + tuple((t, 1) for t in range(2, N_TILES))
 WARM_UP = (128, 256, 512, 512)
 TAIL = 3 * J // 8
 BLOCKS = 16
 GATE_BYTES = 4 * T
 KB = 1024
 GATE_AT = (4, 8, 13, 19, 23, 27, 31, 35)
-X_AT = (18, 26, 33)
+X_AT = (18, 26, 31, 35)
 EARLY = N // 2
 WT_COL, WX_COL, V_COL = 0, N, 2 * N
 
@@ -96,6 +96,7 @@ def tile_list_tiert_gate_kernel(
         load_scale_rows(planes, wx_scales[0], WX_COL)
         load_scale_rows(planes, wt_scales[0], WT_COL)
         load_x(2)
+        load_x(3)
         wx_rows = wx_words[0].rearrange("p n i -> p (n i)")
         load_words(wx[0], wx_rows[:, 0 : PACK * EARLY])
         load_words(wt[0], wt_words[0][:, 0 : 2 * EARLY])
@@ -284,8 +285,8 @@ def tile_list_tiert_gate_kernel(
         quantize_x(3, 1)
         quantize_rest(0, 2)
         subtract(2)
-        subtract(3)
         load_gates(6)
+        subtract(3)
         load_gates(7)
         quantize_rest(2, 1)
         quantize_rest(3, 1)

from contextlib import ExitStack

import concourse.mybir as mybir

K, L, N, T, J = 512, 512, 1024, 1024, 512
FLOPS = 2 * (K * N * J + 2 * L * N * J + L * L * J)

F32 = mybir.dt.float32
BF16 = mybir.dt.bfloat16
I32 = mybir.dt.int32
U32 = mybir.dt.uint32
U16 = mybir.dt.uint16
U8 = mybir.dt.uint8
FP8X4 = mybir.dt.float8_e4m3fn_x4
FP4X4 = mybir.dt.float4_e2m1fn_x4
MULT = mybir.AluOpType.mult
SUBTRACT = mybir.AluOpType.subtract

P = 128
PACK = 4
CHUNK = 128
HALF = J // 2
N_TILES = N // P
X_LOADS = ((0, 1), (1, 1), (2, 1), (3, 1))
STORE_GROUPS = ((0, 2),) + tuple((t, 1) for t in range(2, N_TILES))
WARM_UP = (128, 256, 512, 512)
TAIL = 3 * J // 8
BLOCKS = 16
GATE_BYTES = 4 * T
KB = 1024
GATE_AT = (4, 8, 13, 19, 23, 27, 31, 35)
X_AT = (18, 26, 31, 35)
EARLY = N // 2
WT_COL, WX_COL, V_COL = 0, N, 2 * N


def tile_list_tiert_gate_kernel(
    tc, tab_words, tab_scales, wt_words, wt_scales, x, wx_words, wx_scales, gT, offs, out
):
    nc = tc.nc
    with ExitStack() as ctx:
        keep = ctx.enter_context(tc.tile_pool(name="keep", bufs=1))
        stream = ctx.enter_context(tc.tile_pool(name="stream", bufs=1))
        psum = ctx.enter_context(tc.psum_pool(name="psum", bufs=8))

        offsets = keep.tile([P, J // 16], U16, name="offsets")
        table = stream.tile([P, T], U32, name="table", align_bytes=256, offset=21 * KB // 2)
        table_sc = stream.tile([P, T + 4], U8, name="table_sc", align_bytes=256, offset=0)
        wt = (
            keep.tile([P, 2 * EARLY], U8, name="wt_early", align_bytes=256),
            stream.tile([P, 2 * EARLY], U8, name="wt_late", align_bytes=256, offset=12 * KB),
        )
        planes = keep.tile([P, 2 * N + J + 4], U8, name="planes", align_bytes=256)
        wx = (
            keep.tile([P, EARLY], U32, name="wx_early", align_bytes=256),
            stream.tile([P, EARLY], U32, name="wx_late", align_bytes=256, offset=17 * KB),
        )
        x_raw = [
            stream.tile(
                [P, PACK, count * CHUNK],
                F32,
                name="x_raw%d" % first,
                align_bytes=256,
                offset=X_AT[k] * KB,
            )
            for k, (first, count) in enumerate(X_LOADS)
        ]
        picked_sc = stream.tile([P, J], U8, name="picked_sc", align_bytes=256, offset=GATE_BYTES)
        gates = [
            stream.tile([P, T], F32, name="gates%d" % t, align_bytes=256, offset=GATE_AT[t] * KB) for t in range(N_TILES)
        ]

        for plane in (table_sc, planes):
            nc.vector.memset(plane[:].bitcast(I32), 0)

        x_rows = x.rearrange("(p i) j -> p i j", i=PACK)

        def load_x(k):
            first, count = X_LOADS[k]
            nc.sync.dma_start(out=x_raw[k][:], in_=x_rows[:, :, first * CHUNK : (first + count) * CHUNK])

        def load_words(tile, words):
            nc.sync.dma_start(out=tile[:].bitcast(I32), in_=words.bitcast(I32))

        def load_scale_rows(plane, rows, column):
            nc.sync.dma_start(out=plane[0:BLOCKS, column : column + N].bitcast(I32), in_=rows.bitcast(I32))

        def load_gates(t):
            nc.sync.dma_start(out=gates[t][:], in_=gT[t * P : (t + 1) * P, :])

        load_x(0)
        nc.sync.dma_start(out=offsets[:], in_=offs)
        load_scale_rows(table_sc, tab_scales[0], 0)
        load_x(1)
        load_words(table, tab_words[0].rearrange("p t i -> p (t i)"))
        load_scale_rows(planes, wx_scales[0], WX_COL)
        load_scale_rows(planes, wt_scales[0], WT_COL)
        load_x(2)
        load_x(3)
        wx_rows = wx_words[0].rearrange("p n i -> p (n i)")
        load_words(wx[0], wx_rows[:, 0 : PACK * EARLY])
        load_words(wt[0], wt_words[0][:, 0 : 2 * EARLY])

        width = P * PACK
        pick = stream.tile([P, PACK * width + 32], BF16, name="pick", align_bytes=256, offset=GATE_BYTES - 1024)
        last = (PACK - 1) * width
        source = pick[:, last : last + width + 32]
        nc.gpsimd.memset(source.bitcast(I32), 0)
        nc.gpsimd.affine_select(
            out=source.bitcast(F32),
            in_=source.bitcast(F32),
            compare_op=mybir.AluOpType.not_equal,
            fill=1.0,
            base=1,
            pattern=[[-1, (width + 32) // 2]],
            channel_multiplier=2,
        )
        for i in range(PACK - 1):
            first = PACK - 1 - i
            nc.vector.tensor_copy(out=pick[:, i * width : (i + 1) * width], in_=source[:, first : first + width])
        pick_codes = keep.tile([P, PACK * P], U32, name="pick_codes", align_bytes=256)
        pick_sc = keep.tile([P, PACK * P], U8, name="pick_sc", align_bytes=256)
        nc.vector.quantize_mx(out=pick_codes[:].bitcast(FP8X4), scales=pick_sc[:], in_=pick[:, 0 : PACK * width])

        warm = psum.tile([P, J], F32, name="bank")
        for columns in WARM_UP:
            nc.tensor.matmul_mx(
                out=warm[:, 0:columns],
                lhsT=pick_codes[:, 0:P].bitcast(FP8X4),
                lhsT_scale=pick_sc[:, 0:P],
                rhs=pick_codes[:, 0:columns].bitcast(FP8X4),
                rhs_scale=pick_sc[:, 0:columns],
                start=True,
                stop=True,
            )

        v_codes = stream.tile([P, J], U32, name="v_codes", align_bytes=256, offset=0)
        v_sc = planes[:, V_COL : V_COL + J]
        xq_in = keep.tile([P, HALF, PACK], BF16, name="xq_in", align_bytes=256)
        xr_in = keep.tile([P, J, PACK], BF16, name="xr_in", align_bytes=256)
        xq_codes = stream.tile([P, J], U32, name="xq_codes", align_bytes=256, offset=4 * J)
        xq_sc = keep.tile([P, J], U8, name="xq_sc", align_bytes=256)
        xr_codes = keep.tile([P, J], U32, name="xr_codes", align_bytes=256)
        xr_sc = keep.tile([P, J], U8, name="xr_sc", align_bytes=256)
        decoded = {}

        def cols_of(c):
            return slice(c * CHUNK, (c + 1) * CHUNK)

        def x_chunk(c):
            for k, (first, count) in enumerate(X_LOADS):
                if first <= c < first + count:
                    return x_raw[k][:, :, cols_of(c - first)].rearrange("p i (g e) -> p g i e", e=2)

        def round_x(c):
            nc.scalar.copy(out=xq_in[:, cols_of(c % 2), :].rearrange("p (g e) i -> p g i e", e=2), in_=x_chunk(c))

        def quantize_x(first, count):
            cols = slice(first * CHUNK, (first + count) * CHUNK)
            inner = (first % 2) * CHUNK
            nc.vector.quantize_mx(
                out=xq_codes[:, cols].bitcast(FP8X4),
                scales=xq_sc[:, cols],
                in_=xq_in[:, inner : inner + count * CHUNK, :].rearrange("p j i -> p (j i)"),
            )
            for c in range(first, first + count):
                decode(c)

        def decode(c):
            bank = psum.tile([P, PACK, CHUNK], F32, name="bank")
            decoded[c] = bank
            for i in range(PACK):
                m_cols = slice(i * P, (i + 1) * P)
                nc.tensor.matmul_mx(
                    out=bank[:, i, :],
                    lhsT=pick_codes[:, m_cols].bitcast(FP8X4),
                    lhsT_scale=pick_sc[:, m_cols],
                    rhs=xq_codes[:, cols_of(c)].bitcast(FP8X4),
                    rhs_scale=xq_sc[:, cols_of(c)],
                    start=True,
                    stop=True,
                )

        def subtract(c):
            nc.vector.tensor_tensor(
                out=xr_in[:, cols_of(c), :].rearrange("p (g e) i -> p g i e", e=2),
                in0=x_chunk(c),
                in1=decoded[c][:].rearrange("p i (g e) -> p g i e", e=2),
                op=SUBTRACT,
            )

        def quantize_rest(first, count):
            cols = slice(first * CHUNK, (first + count) * CHUNK)
            nc.vector.quantize_mx(
                out=xr_codes[:, cols].bitcast(FP8X4),
                scales=xr_sc[:, cols],
                in_=xr_in[:, cols, :].rearrange("p j i -> p (j i)"),
            )

        def gather_scales(lo, hi):
            nc.vector.tensor_copy(out=picked_sc[:, lo:hi], in_=table_sc[:, 0:T].indirect(offsets[:, lo // 16 : hi // 16]))

        def spread_scale_rows():
            nc.vector.tensor_copy(out=planes[0:32, V_COL : V_COL + J].bitcast(I32), in_=picked_sc[0:32, :].bitcast(I32))
            for q in range(1, 4):
                nc.sync.dma_start(
                    out=planes[32 * q : 32 * q + 4, 0 : V_COL + J].bitcast(I32),
                    in_=planes[4 * q : 4 * q + 4, 0 : V_COL + J].bitcast(I32),
                )

        def gather_words(lo, hi):
            nc.vector.tensor_copy(out=v_codes[:, lo:hi], in_=table[:].indirect(offsets[:, lo // 16 : hi // 16]))

        banks = {}

        def one_pass(t, w_codes, first, codes, sc, lo, c0, c1, start, stop):
            if start:
                banks[t, lo] = psum.tile([P, J], F32, name="bank")
            nc.tensor.matmul_mx(
                out=banks[t, lo][:, c0:c1],
                lhsT=w_codes,
                lhsT_scale=planes[:, first + t * P : first + (t + 1) * P],
                rhs=codes[:, c0:c1].bitcast(FP8X4),
                rhs_scale=sc[:, c0:c1],
                start=start,
                stop=stop,
            )
            if stop:
                nc.scalar.copy(out=sums[t][:, lo:c1], in_=banks[t, lo][:, lo:c1])

        def first_tier(t, lo, hi):
            wx_codes = wx[t // 4][:, (t % 4) * P : (t % 4 + 1) * P].bitcast(FP8X4)
            one_pass(t, wx_codes, WX_COL, xq_codes, xq_sc, lo, lo, hi, True, False)

        def table_part(t, lo, hi, stop=False):
            wt_codes = wt[t // 4][:, 2 * (t % 4) * P : 2 * (t % 4 + 1) * P].bitcast(FP4X4)
            step = J if hi - lo == J else CHUNK
            for c0 in range(lo, hi, step):
                one_pass(t, wt_codes, WT_COL, v_codes, v_sc, lo, c0, c0 + step, False, stop and c0 + step == hi)

        def second_tier(t, lo, hi, stop=True):
            wx_codes = wx[t // 4][:, (t % 4) * P : (t % 4 + 1) * P].bitcast(FP8X4)
            one_pass(t, wx_codes, WX_COL, xr_codes, xr_sc, lo, lo, hi, False, stop)

        sums = [keep.tile([P, J], F32, name="sums%d" % t, align_bytes=256) for t in range(N_TILES)]
        gated = {}
        for first, count in STORE_GROUPS:
            group = keep.tile([P, count, J], F32, name="gated%d" % first, align_bytes=256)
            for k in range(count):
                gated[first + k] = (group, first, count)

        def gate_part(t, lo, hi):
            nc.vector.tensor_tensor(
                out=gated[t][0][:, t - gated[t][1], lo:hi],
                in0=gates[t][:].indirect(offsets[:, lo // 16 : hi // 16]),
                in1=sums[t][:, lo:hi],
                op=MULT,
            )

        def store(t, lo, hi):
            group, first, count = gated[t]
            if t == first + count - 1:
                rows = out[first * P : (first + count) * P, lo:hi].rearrange("(g p) j -> p g j", p=P)
                nc.sync.dma_start(out=rows, in_=group[:, :, lo:hi])

        round_x(0)
        round_x(1)
        gather_scales(0, J)
        quantize_x(0, 2)
        spread_scale_rows()
        load_gates(0)
        round_x(2)
        round_x(3)
        gather_words(0, J)
        load_gates(1)
        load_gates(2)
        load_words(wt[1], wt_words[0][:, 2 * EARLY : 2 * N])
        subtract(0)
        load_words(wx[1], wx_rows[:, PACK * EARLY : PACK * N])
        load_gates(3)
        quantize_x(2, 1)
        subtract(1)
        load_gates(4)
        load_gates(5)
        quantize_x(3, 1)
        quantize_rest(0, 2)
        subtract(2)
        load_gates(6)
        subtract(3)
        load_gates(7)
        quantize_rest(2, 1)
        quantize_rest(3, 1)
        parts = ((0, 0, HALF), (1, 0, HALF), (0, HALF, 3 * CHUNK), (0, 3 * CHUNK, J), (1, HALF, J))
        for part in parts[:2]:
            first_tier(*part)
            table_part(*part)
        for part in parts[:2]:
            second_tier(*part)
        for part in parts[2:]:
            first_tier(*part)
            table_part(*part)
        for part in parts[2:]:
            second_tier(*part)
        gate_part(0, 0, HALF)
        gate_part(0, HALF, J)
        store(0, 0, J)
        gate_part(1, 0, J)
        store(1, 0, J)
        for t in range(2, N_TILES):
            first_tier(t, 0, J)
            table_part(t, 0, J)
            second_tier(t, 0, J)
            edges = (0, J - TAIL, J) if t == N_TILES - 1 else (0, J)
            for k in range(len(edges) - 1):
                gate_part(t, edges[k], edges[k + 1])
                store(t, edges[k], edges[k + 1])
